import numpy as np, ml_dtypes
CORES = [6,15,38,47]
N = 4
BF = ml_dtypes.bfloat16
def gentries(a):
    return np.ascontiguousarray(a.reshape(8, 16, -1).transpose(0, 2, 1)).reshape(8, -1)
def gtable(e):
    e = np.asarray(e); return np.ascontiguousarray(e.reshape(8, -1, 16).transpose(0, 2, 1)).reshape(128, -1).astype(np.int32)
C, M, G, T, TH, S = 8192, 1024, 256, 4, 10, 32
def parts(rng):
    R = rng.integers(0, 256, (N, 8, 16, C)); P = rng.integers(0, M, (N, 8, 16, M)); O = rng.integers(0, M, (N, 8, 16, M))
    z = (256 * rng.choice(np.array([0.6, 0.8, 1.0]), (N, 8, 1, G)) * rng.random((N, 8, 16, G))).astype(np.int64)
    return R, P, O, z, rng.integers(0, M, (N, 8, G)), rng.integers(1, 257, (N, 8, 16))
def pack(R, P, O, z, mv, w):
    P = np.array(P); O = np.array(O); P[:, :, 0] = np.arange(M); O[:, :, 0] = np.arange(M)
    return {"strat": R.reshape(N, 128, C).astype(np.float32).astype(BF), "vp": P.reshape(N, 128, M).astype(np.int32), "vo": O.reshape(N, 128, M).astype(np.int32),
            "z0": z.reshape(N, 128, G).astype(np.float32).astype(BF), "mv": np.stack([gtable(a) for a in mv]), "wt": w.reshape(N, 128, 1).astype(np.int32)}
def plant(rng, R, P, O, z, mv, w):
    h = 17 - TH; m = np.arange(M)
    w[:, :, 13] = 16; w[:, :, 14] = 1; w[:, 2, :13] = np.maximum(w[:, 2, :13], 160)
    for r in range(N):
        q = (r + 1) % N
        for g in range(8):
            own = rng.permutation(M)[:12]; i = 1 + rng.permutation(G - 17)[:5]; wq = w[q, g]
            for e in range(4):
                a = int(i[e]); mv[r, g, a] = own[e]; P[r, g, 3 + 4 * e, own[e]] = M - 1
                z[r, g, :h, a] = 255; z[r, g, 13:15, a] = 0
                d = (4065 - int(np.sum(wq * z[r, g, :, a]))) & 4095
                z[r, g, 13, a] = d >> 4; z[r, g, 14, a] = d & 15
            if g == 2:
                left = 2 ** 19
                for j in list(range(13)) + [15, 13, 14]:
                    n = min(255, left // int(wq[j])); z[r, g, j, int(i[4])] = n; left -= n * int(wq[j])
            end = G - 15 + 2 * np.arange(8); mv[r, g, end] = own[4:]
            z[r, g, :h, G - 15::2] = 255
            u = np.sum(wq[:, None] * z[r, g], axis=0) & 4095; p0 = int(u[0]) & (S - 1)
            R[q, g, :, p0] = 255 * rng.integers(0, 2, 16)
            ad = (((m[:, None] * u[end][None, :]) >> 5) + m[:, None] + 37 * 15) & (C - 1)
            for e in range(8):
                good = np.flatnonzero(ad[:, e] == p0)
                if len(good): P[r, g, 15, own[4 + e]] = rng.choice(good)
    return R, P, O, z, mv, w
def setup_inputs(rng):
    return pack(*plant(rng, *parts(rng)))
def corner(rng, first):
    R, P, O, z, mv, w = parts(rng); R = np.maximum(R, 1); m = np.arange(M)[None, :]; j = np.arange(16)[:, None]
    forms = [m + 0 * j, np.maximum(m - j, 0), np.minimum(m + j, M - 1), np.where((m + j) % 2 == 0, 0, M - 1)]
    P = np.stack([np.stack([forms[(g + r) % 4] for g in range(8)]) for r in range(N)])
    O = np.stack([np.stack([forms[(g + r + 1 + g // 4) % 4] for g in range(8)]) for r in range(N)])
    cnt = np.array([255, 256, 1024, 512, 257, 511, 1, 8 * G - 1, 8 * G, 0, 1536, 4 * G, 6 * G, 8 * G - 256, 1023, 1025])[first * N:first * N + N]
    cnt = np.roll(cnt, int(rng.integers(0, N)))
    for r in range(N):
        for g in range(8):
            e = (g + r) % 3
            if e == 0: mv[r, g] = rng.choice(np.array([0, M - 1]), G)
            elif e == 1: mv[r, g] = rng.integers(0, M)
            else: mv[r, g] = rng.permutation(M)[:G]
        hit = np.zeros(8 * G, bool); hit[rng.permutation(8 * G)[:int(cnt[r])]] = True
        z[r] = np.where(hit.reshape(8, 1, G), 0, 255)
    w[:, 1] = 1; w[:, 5] = 256
    return pack(R, P, O, z, mv, w)
def setup_inputs_corners(rng):
    return corner(rng, 0)
def setup_inputs_corners_two(rng):
    return corner(rng, 1)
def setup_inputs_ends(rng):
    R = np.where(rng.random((N, 8, 16, C)) < rng.choice(np.array([0.1, 0.5, 0.75, 0.9]), (N, 8, 1, C)), 255, 0)
    z = np.where(rng.random((N, 8, 16, G)) < rng.choice(np.array([0.05, 0.3, 0.8]), (N, 8, 1, G)), 255, 0)
    P = (M - 1) * rng.integers(0, 2, (N, 8, 16, M)); O = (M - 1) * rng.integers(0, 2, (N, 8, 16, M)); mv = (M - 1) * rng.integers(0, 2, (N, 8, G))
    w = np.where(rng.random((N, 8, 16)) < 0.5, 256, 1)
    mv[:, :, G - 1] = M - 1; P[:, :, 15, M - 1] = M - 1; O[:, :, 15, M - 1] = M - 1
    w[:, 0] = 256; R[:, 0] = np.where(rng.random((N, 1, C)) < 0.5, 255, 0); z[:, 0, :, G - 1] = 255; z[:, 0, :, 0] = 0
    w[:, 5:] = 256; w[:, 5:, 15] = 1
    c = np.zeros(16, np.int64); c[3] = 255; c[15] = 255
    x8 = np.array([0, 1, 2, 4, 5, 6, 7, 8]); y4 = np.array([9, 10, 11, 12])
    for g in (6, 7):
        hot = ((np.arange(C) >> 7) + g) % 2 == 1
        R[:, g] = c[None, :, None]
        R[:, g, x8] = np.where(hot, 192, 64 * rng.integers(0, 2, (N, 1, C))); R[:, g, y4] = np.where(hot, 128, 0)
        z[:, g, :, 1::2] = c[None, :, None]; z[:, g, :, G - 1] = c[None, :]
    R[:, 5] = 0; R[:, 5, 15] = 255; R[:, 5, y4] = 128 * rng.integers(0, 2, (N, 1, C))
    R[:, 5, x8, C - 1] = 192; R[:, 5, y4, C - 1] = 128
    z[:, 5] = 0; z[:, 5, 15] = 255
    m = np.arange(M); f = ((m * 255) >> 5) + m
    for j in range(1, 14):
        near = m[((f + 37 * (j + 1)) & (C - 1)) >= C - 256]
        P[:, 5, j] = rng.choice(near, (N, M)); O[:, 5, j] = rng.choice(near, (N, M))
    P[:, 5, 14:] = rng.integers(0, M, (N, 2, M)); O[:, 5, 14:] = rng.integers(0, M, (N, 2, M))
    mv[:, 5] = np.argsort(rng.random((N, M)), axis=1)[:, :G]; mv[:, 5, G - 1] = M - 1
    keep = np.array(R[3, 5])
    z[1, :, :17 - TH] = 255; z[2, :, :TH] = 0; R[3, :, :TH] = 255
    a0 = f[mv[2, 5]] & (C - 1); keep[np.ix_(x8, a0)] = 192; keep[np.ix_(y4, a0)] = 128; R[3, 5] = keep
    return pack(R, P, O, z, mv, w)
def setup_inputs_spread(rng):
    R = np.minimum((np.exp2(8 * rng.random((N, 8, 1, C))) * rng.random((N, 8, 16, C))).astype(np.int64), 255)
    z = np.minimum((np.exp2(8 * rng.random((N, 8, 1, G))) * rng.random((N, 8, 16, G))).astype(np.int64), 255)
    P = np.minimum((M * rng.random((N, 8, 16, M)) ** 3).astype(np.int64), M - 1); O = np.minimum((M * rng.random((N, 8, 16, M)) ** 3).astype(np.int64), M - 1)
    mv = np.minimum((M * rng.random((N, 8, G)) ** 2).astype(np.int64), M - 1)
    w = np.minimum(np.maximum(np.rint(np.exp2(8 * rng.random((N, 8, 16)))).astype(np.int64), 1), 256)
    v0 = [v for v in range(M + G * (T - 2), M + G * (T - 1)) if (-(2 ** 22)) % v < 32][0]
    u0 = (2 ** 22 + v0 - 1) // v0 - 32
    r = int(rng.integers(0, N)); q = (r + 1 + (T - 1) % (N - 1)) % N; p = (r + 1 + (T - 2) % (N - 1)) % N
    R[q, :, :17 - TH] = 0
    for g in (1, 3, 4, 6):
        w[q, g, 13] = 16; w[q, g, 14] = 1
        c = rng.integers(0, 256, 16); c[13:15] = 0
        d = (u0 - int(np.sum(w[q, g] * c))) & 4095
        c[13] = d >> 4; c[14] = d & 15
        R[p, g] = c[:, None]
        R[q, g, 15] = 0; R[q, g, 15, 0] = 255
    return pack(R, P, O, z, mv, w)
def setup_inputs_ties(rng):
    R, P, O, z, mv, w = parts(rng)
    b = rng.integers(0, 255, (8, 16)); b[0] = 0; b[6] = 254
    share = rng.permutation(np.array([0.02, 0.04, 0.07, 0.1, 0.15, 0.2, 0.3, 0.5])).reshape(1, 8, 1, 1)
    cnt = np.where(rng.random((N, 8, 1, C)) < share, rng.choice(np.array([TH, TH, TH, TH + 1, 16]), (N, 8, 1, C)), rng.choice(np.array([TH - 1, TH - 1, TH - 1, 0]), (N, 8, 1, C)))
    R = b[None, :, :, None] + (np.argsort(rng.random((N, 8, 16, C)), axis=2) < cnt)
    z = b[None, :, :, None] + (rng.random((N, 8, 1, G)) < 0.125) + np.zeros((N, 8, 16, G), np.int64)
    return pack(R, P, O, z, mv, w)
def check_inputs(d):
    bad = []
    for k, lo, hi in (("strat", 0, 255), ("vp", 0, M - 1), ("vo", 0, M - 1), ("z0", 0, 255), ("mv", 0, M - 1), ("wt", 1, 256)):
        a = np.asarray(d[k]).astype(np.float64)
        if not (np.min(a) >= lo and np.max(a) <= hi): bad.append("range of " + k)
        elif np.any(a != np.floor(a)): bad.append("whole numbers in " + k)
    for k in ("vp", "vo"):
        if np.any(np.asarray(d[k]).reshape(-1, 8, 16, M)[:, :, 0] != np.arange(M)): bad.append("row 0 of the views in " + k)
    return bad
def reference(strat, vp, vo, z0, mv, wt):
    R = strat.astype(np.float32).astype(np.int32).reshape(N, 8, 16, C); z = z0.astype(np.float32).astype(np.int32).reshape(N, 8, 16, G)
    w = wt.astype(np.int32).reshape(N, 8, 16, 1); v = np.stack([gentries(a) for a in mv]).astype(np.int64)
    room = np.zeros((N, 8, 16, G * T), np.int32)
    views = [np.concatenate([a.astype(np.int32).reshape(N, 8, 16, M), room], axis=3) for a in (vp, vo)]
    count = np.zeros(N, np.int64); kk = np.arange(16)[None, None, :, None]; verdicts = np.zeros((N, 8, T, G), np.int64)
    for t in range(T):
        mover, other = views[t % 2], views[1 - t % 2]
        q = (np.arange(N) + 1 + t % (N - 1)) % N
        L = np.take_along_axis(mover, v[:, :, None, :], 3).astype(np.int64)
        u = np.add.reduce(w[q] * z, axis=2).astype(np.int64) & 4095
        ad = (((L * u[:, :, None, :]) >> 5) + L + 37 * kk + (count[q] & 255)[:, None, None, None]) & (C - 1)
        Y = np.take_along_axis(R[q], ad.reshape(N, 8, 1, 16 * G), 3).reshape(N, 8, 16, 16, G)
        hit = np.add.reduce((Y > z[:, :, :, None, :]).astype(np.int32), axis=2) >= TH
        hit[:, :, 15] = True
        kap = np.argmax(hit, axis=2)
        use = (kk <= kap[:, :, None, :])[:, :, None]
        z = (np.maximum.reduce(np.where(use, Y, 0), axis=3) + np.minimum.reduce(np.where(use, Y, 255), axis=3)) >> 1
        z = z.astype(np.int32)
        if t < T - 1:
            place = S * np.arange(G) + (u & (S - 1))
            for r in range(N):
                ix = np.repeat(place[r][:, None, :], 16, axis=1); mine = R[int(q[r])]
                np.put_along_axis(mine, ix, (np.take_along_axis(mine, ix, 2) + z[r]) >> 1, 2)
        count[q] = np.add.reduce((kap < 15).reshape(N, 8 * G).astype(np.int64), axis=1)
        named = np.take_along_axis(L, kap[:, :, None, :], 2)
        resumed = np.take_along_axis(other, named, 3)
        n0 = M + G * t; n = np.zeros((N, 8, 1, G), np.int64) + n0 + np.arange(G)
        mover[..., n0:n0 + G] = np.concatenate([n, L[:, :, :15]], axis=2)
        other[..., n0:n0 + G] = np.concatenate([n, resumed[:, :, :15]], axis=2)
        v = n[:, :, 0]; verdicts[:, :, t] = kap
    e = M + G * (T - 1)
    return {"yp": views[0][..., e:e + G].reshape(N, 128, G).astype(np.float32), "yo": views[1][..., e:e + G].reshape(N, 128, G).astype(np.float32),
            "yz": z.reshape(N, 128, G).astype(np.float32).astype(BF), "yk": verdicts.reshape(N, 8, T * G).astype(np.float32)}

@@ -1,0 +1,731 @@
+import math
+import numpy as np
+from concourse.bass import DstId, RemoteDMATransfer
+from concourse.mybir import dt, AluOpType, AxisListType, ActivationFunctionType
+
+A = AluOpType
+COPY = ActivationFunctionType.Copy
+IDN = ActivationFunctionType.Identity
+MAGIC = 12582912.0
+
+SUB = {0: [0, 48, 128], 1: [0, 64, 128]}
+
+
+def _scratch():
+    s = {}
+
+    def sb(name, n, d):
+        s[name] = ("sbuf", [128, n], d)
+    f, b, i, u, h = "float32", "bfloat16", "int32", "uint16", "float16"
+    sb("R", 8192, b)
+    for k in range(2):
+        sb("Y%d" % k, 2048, b); sb("B%d" % k, 2048, b); sb("HI%d" % k, 2048, b); sb("LO%d" % k, 2048, b)
+        sb("al%d" % k, 128, u); sb("nM%d" % k, 128, f); sb("nb%d" % k, 128, b); sb("pr%d" % k, 128, f)
+        sb("aI%d" % k, 128, i); sb("aJ%d" % k, 128, i); sb("rm%d" % k, 128, b); sb("st%d" % k, 128, h)
+        sb("ML%d" % k, 128, h); sb("hs%d" % k, 128, b); sb("ls%d" % k, 128, b)
+        sb("rn%d" % k, 128, b)
+        for p in range(2):
+            sb("L%d%d" % (p, k), 128, f)
+    for t in range(4):
+        sb("MSG%d" % t, 32, u); sb("zo%d" % t, 256, b); sb("zr%d" % t, 256, b); sb("HM%d" % t, 32, u)
+        sb("it%d" % t, 256, f); sb("N%d" % t, 256, f); sb("NF%d" % t, 256, h)
+        if t:
+            sb("LR%d" % t, 32, u)
+        if t < 3:
+            sb("rb%d" % t, 16, i)
+    sb("zf", 256, b); sb("rMP2", 128, f); sb("rMP6", 128, f)
+    for n in ("uI", "uJ", "uK"):
+        sb(n, 16, i)
+    sb("UL", 16, u); sb("old", 256, b)
+    for n, w in (("OB", 1024), ("PC", 1280), ("OA", 1536), ("SP", 1792)):
+        sb(n, w, f)
+    for n in ("oS", "pS", "rOB", "rPC", "rOA"):
+        sb(n, 1024, h)
+    for n in ("vpI", "voI"):
+        sb(n, 1024, i)
+    sb("mvI", 16, i); sb("mvu", 16, u); sb("wI", 1, i); sb("zn", 256, b); sb("zs", 256, b)
+    sb("L0n", 256, f)
+    for n in ("L0h", "L0A", "L0C", "L1A", "L2H", "L3h", "L3r"):
+        sb(n, 256, h)
+    for n in ("ip", "p16", "pg", "i1", "i2", "i3", "i4", "i5", "i6", "i7", "cAi", "cAj"):
+        sb(n, 1, i)
+    for n in ("pf", "p16f", "pgf", "pg16", "p1", "p2", "k15", "k14", "m0", "m1", "wf", "ck", "cA", "cR", "f1", "f2", "f3",
+              "f4", "f5", "f6", "g1", "g2", "g3", "g4", "g5", "g6", "x128"):
+        sb(n, 1, f)
+    sb("fr", 144, f); sb("Dn", 144, b); sb("Dw", 144, b); sb("D16", 144, h)
+    for n in ("I1", "I2", "I4", "I4k", "bda", "bdb", "BD", "WB", "cz", "cr", "cu", "c32", "ones", "nones"):
+        sb(n, 128, b)
+    sb("ik", 128, f); sb("ck16", 128, f)
+    for n in ("Sh1", "Sh2"):
+        sb(n, 128, b)
+    sb("EX", 2048, b); sb("ind", 16, f); sb("s0", 2048, b); sb("s1", 2048, b)
+    sb("q1", 128, f); sb("Bq", 128, f); sb("Br", 128, f); sb("Bc", 128, f); sb("iy", 128, f); sb("i8", 8, f); sb("k16", 8, f)
+    sb("jp", 96, f)
+    sb("pl", 16, u); sb("yc", 64, i); sb("yq", 64, i); sb("ye", 64, i); sb("yb", 64, i); sb("yd", 64, i); sb("yl", 64, u)
+    sb("hk", 128, f); sb("kall", 64, b)
+    sb("ykr", 1024, f); sb("ykr3", 256, f); sb("ykn", 1024, f); sb("ypb", 256, f); sb("yob", 256, f)
+    return s
+
+
+_ALL = _scratch()
+_PACK = {}
+
+
+def _pack():
+    out, width = {}, {}
+    size = {"float32": 4, "int32": 4, "bfloat16": 2, "uint16": 2, "float16": 2}
+    for name, (w, sh, d) in _ALL.items():
+        if sh[1] <= 256:
+            al = 32 // size[d]
+            o = width.get(d, 0)
+            _PACK[name] = ("pk_" + d, o, sh[1])
+            width[d] = o + -(-sh[1] // al) * al
+        else:
+            out[name] = (w, sh, d)
+    for d, w in width.items():
+        out["pk_" + d] = ("sbuf", [128, w], d)
+    for k in range(8):
+        out["P%d" % k] = ("psum", [128, 512], "float32")
+    return out
+
+
+SCRATCH = _pack()
+_ARR = ["aL0", "az0", "aOB", "aPC", "aL0C", "aOA", "aL3"] + ["al%d%d" % (t, h) for t in (1, 2, 3) for h in (0, 1)] \
+    + ["az%d%d" % (t, h) for t in (1, 2, 3, 4) for h in (0, 1)] + ["ah0", "ah1", "ah2", "ah30", "ah31", "aho"]
+SEMAPHORES = ["sV", "sT", "sS", "sG", "ls"] + ["d%d" % k for k in range(20)] + _ARR
+
+
+def rank_program(g, core, T, topo):
+    q = T.rank_of(core)
+    if q is None:
+        return
+    ENG = {"V": g.vector, "T": g.tensor, "S": g.scalar, "G": g, "Y": g.sync}
+    QSEM = {"V": "sV", "T": "sT", "S": "sS", "G": "sG"}
+    cnt = {k: 0 for k in QSEM}
+    clock = {k: {} for k in ENG}
+    last, readers = {}, {}
+    used = {}
+    dn = [0]
+
+    def X(name, a=None, b=None, step=None, rows=None):
+        buf, o, w = _PACK.get(name, (name, 0, None))
+        t = T[buf]
+        if w is None:
+            w = t.shape[1]
+        a = 0 if a is None else a
+        b = w if b is None else b
+        r = slice(0, 128) if rows is None else rows
+        if step is None:
+            return t[r, o + a:o + b]
+        return t[r, o + a:o + b:step]
+
+    def wait(qn, tok):
+        sem, val, snap, _ = tok
+        ck = clock[qn]
+        if ck.get(sem, 0) >= val:
+            return
+        ENG[qn].wait_ge(T.sem[sem], val)
+        ck[sem] = val
+        for s, v in snap.items():
+            if ck.get(s, 0) < v:
+                ck[s] = v
+
+    def before(qn, R, W):
+        for k in R:
+            if k in last:
+                wait(qn, last[k])
+            if k[0] == "P" and k[1].isdigit():
+                for e, tok in readers.get(k, {}).items():
+                    if e != qn:
+                        wait(qn, tok)
+        for k in W:
+            if k in last and (last[k][3] != qn or qn == "Y"):
+                wait(qn, last[k])
+            for e, tok in readers.get(k, {}).items():
+                if e != qn:
+                    wait(qn, tok)
+
+    def after(qn, tok, R, W):
+        for k in R:
+            readers.setdefault(k, {})[qn] = tok
+        for k in W:
+            last[k] = tok
+            readers[k] = {}
+
+    prog, cur = [], [0.0]
+
+    def at(stage):
+        cur[0] = float(stage)
+
+    def op(*a):
+        prog.append((cur[0], len(prog), op_now, a))
+
+    def dma(*a):
+        prog.append((cur[0], len(prog), dma_now, a))
+
+    def send(*a):
+        prog.append((cur[0], len(prog), send_now, a))
+
+    def op_now(qn, calls, R, W):
+        before(qn, R, W)
+        calls = calls if isinstance(calls, list) else [calls]
+        for c in calls:
+            ins = c()
+        cnt[qn] += 1
+        ins.then_inc(T.sem[QSEM[qn]], 1)
+        used[QSEM[qn]] = cnt[qn]
+        after(qn, (QSEM[qn], cnt[qn], dict(clock[qn]), qn), R, W)
+
+    def dma_now(qn, out, in_, R, W):
+        before(qn, R, W)
+        sem = "d%d" % dn[0]
+        dn[0] += 1
+        ENG[qn].dma_start(out, in_).then_inc(T.sem[sem], 16)
+        used[sem] = 16
+        after("D" + sem, (sem, 16, dict(clock[qn]), "D" + sem), R, W)
+
+    def send_now(dst, out, in_, sem, R):
+        before("G", R, [])
+        c = T.cores[dst % 4]
+        rid, pid = topo.addr(c)[:2]
+        m = topo.mask(core, c)
+        g.remote_dma(out, in_, T.sem[sem], T.sem.ls, pid, rid, m)
+        used["ls"] = used.get("ls", 0) + len(topo.engines(core, c))
+
+    def arrives(src, sem, key):
+        n = len(topo.engines(T.cores[src % 4], core))
+        used[sem] = n
+        last[key] = (sem, n, {}, "net")
+        readers[key] = {}
+
+    V, PE, S, G = g.vector, g.tensor, g.scalar, g
+
+    def ts(out, i, s1, s2, o0, o1=None):
+        if o1 is None:
+            return lambda: V.tensor_scalar(out, i, s1, None, o0)
+        return lambda: V.tensor_scalar(out, i, s1, s2, o0, o1)
+
+    def tt(out, a, b, o):
+        return lambda: V.tensor_tensor(out, a, b, o)
+
+    def cp(out, a):
+        return lambda: V.tensor_copy(out, a)
+
+    def act(out, a, f=COPY, **kw):
+        return lambda: S.activation(out, a, f, **kw)
+
+    def mm(out, l, r, st=True, sp=True):
+        return lambda: PE.matmul(out, l, r, st, sp)
+
+    def vts(o, i, s1, s2, o0, o1=None, R=()):
+        rd = [i] + [s for s in (s1, s2) if isinstance(s, str)]
+        f = lambda s: X(s) if isinstance(s, str) else s
+        op("V", ts(X(o), X(i), f(s1), f(s2), o0, o1), rd, [o])
+
+    at(-10)
+    dma("Y", X("mvI"), T.mv[:, :], [], ["mvI"])
+    dma("Y", X("vpI"), T.vp[:, :], [], ["vpI"])
+    dma("S", X("zn"), T.z0[:, :], [], ["zn"])
+    dma("S", X("wI"), T.wt[:, :], [], ["wI"])
+    dma("Y", X("R", 0, 4096), T.strat[:, 0:4096], [], ["Ra"])
+    dma("S", X("R", 4096, 8192), T.strat[:, 4096:8192], [], ["R"])
+    dma("Y", X("voI"), T.vo[:, :], [], ["voI"])
+    at(-9)
+
+    def iota(name, pattern, base=0, cm=0, a=None, b=None, integer=False, key=None, early=False):
+        o = X(name, a, b)
+        at0 = cur[0]
+        at(-9.5 if early else at0)
+        if integer:
+            op("G", lambda: G.iota(o, pattern, base, cm), [], [key or name])
+        else:
+            op("G", lambda: G.iota(o, pattern, base, cm, allow_small_or_imprecise_dtypes=True), [], [key or name])
+        at(at0)
+
+    iota("ip", [[0, 1]], 0, 1, integer=True)
+    iota("jp", [[128, 2], [1, 4], [64, 2]], a=0, b=16, key="jp0")
+    vts("p16", "ip", 15, None, A.bitwise_and)
+    vts("g1", "p16", 4.0, None, A.mult)
+    op("V", cp(X("mvu"), X("mvI")), ["mvI"], ["mvu"])
+    op("V", ts(X("pl"), X("jp", 0, 16), X("g1"), None, A.add), ["jp0", "g1"], ["pl"])
+    op("S", act(X("zs"), X("zn").indirect(X("pl"))), ["zn", "pl"], ["zs"])
+    op("V", cp(X("L0n"), X("vpI").indirect(X("mvu"))), ["vpI", "mvu"], ["L0n"])
+    op("V", cp(X("L0h"), X("L0n").indirect(X("pl"))), ["L0n", "pl"], ["L0h"])
+    send(q + 1, X("zr0"), X("zs"), "az0", ["zs"])
+    send(q + 1, X("L0A"), X("L0h"), "aL0", ["L0h"])
+    arrives(q - 1, "az0", "zr0"); arrives(q - 1, "aL0", "L0A")
+
+    iota("fr", [[1, 144]], -16, early=True)
+    vts("pg", "ip", 112, None, A.bitwise_and)
+    op("V", cp(X("pf"), X("ip")), ["ip"], ["pf"])
+    op("V", cp(X("p16f"), X("p16")), ["p16"], ["p16f"])
+    op("V", cp(X("pgf"), X("pg")), ["pg"], ["pgf"])
+    op("V", cp(X("wf"), X("wI")), ["wI"], ["wf"])
+    vts("pg16", "pgf", 16.0, None, A.add)
+    vts("m1", "p16f", 0.0, None, A.is_gt)
+    vts("m0", "p16f", 0.0, None, A.is_equal)
+    vts("ck", "p16f", 1184.0, None, A.mult)
+    fr = X("fr", 16, 144)
+    op("V", ts(X("bda"), fr, X("pgf"), None, A.is_ge), ["fr", "pgf"], ["bda"])
+    op("V", ts(X("bdb"), fr, X("pg16"), None, A.is_lt), ["fr", "pg16"], ["bdb"])
+    op("V", tt(X("BD"), X("bda"), X("bdb"), A.mult), ["bda", "bdb"], ["BD"])
+    vts("WB", "BD", "wf", None, A.mult)
+    op("V", ts(X("I4k"), fr, X("pf"), -4096.0, A.is_equal, A.mult), ["fr", "pf"], ["I4k"])
+    op("V", lambda: V.memset(X("cu", rows=slice(0, 64)), -32.0), [], ["cu"])
+    op("V", lambda: V.memset(X("cu", rows=slice(64, 128)), 2.0 ** -7), [], ["cu"])
+    for n, v in (("ones", 1.0), ("c32", 0.25)):
+        op("V", lambda n=n, v=v: V.memset(X(n), v), [], [n])
+    op("V", ts(X("I1"), fr, X("pf"), None, A.is_equal), ["fr", "pf"], ["I1"])
+    op("V", ts(X("Dw"), X("fr"), X("pgf"), X("wf"), A.is_equal, A.mult), ["fr", "pgf", "wf"], ["Dw"])
+    op("V", ts(X("Dn"), X("fr"), X("pgf"), -1.0, A.is_equal, A.mult), ["fr", "pgf"], ["Dn"])
+    op("V", ts(X("D16"), X("fr"), X("pgf"), None, A.is_equal), ["fr", "pgf"], ["D16"])
+    op("V", ts(X("ind"), X("fr", 16, 32), X("p16f"), None, A.is_equal), ["fr", "p16f"], ["ind"])
+    for x in range(16):
+        op("S", act(X("EX", 128 * x, 128 * x + 128), X("BD"), scale=X("ind", x, x + 1)), ["BD", "ind"], ["EX%d" % x])
+    at(-7.5)
+    op("V", cp(X("pS"), X("vpI")), ["vpI"], ["pS"])
+    at(2)
+    op("V", cp(X("oS"), X("voI")), ["voI"], ["oS"])
+    send(q + 2, X("rOB"), X("oS"), "aOB", ["oS"])
+    send(q + 3, X("rPC"), X("pS"), "aPC", ["pS"])
+    send(q + 3, X("L0C"), X("L0h"), "aL0C", ["L0h"])
+    arrives(q - 2, "aOB", "rOB"); arrives(q + 1, "aPC", "rPC"); arrives(q + 1, "aL0C", "L0C"); arrives(q - 1, "aOA", "rOA")
+
+    at(-7)
+    op("V", lambda: V.memset(X("s0"), 1.0), [], ["s0"])
+    op("V", lambda: V.memset(X("s0", 0, 2048, 16), 0.0), ["s0"], ["s0"])
+    at(2)
+    op("S", act(X("s1"), X("s0"), IDN, bias=256.0, scale=-256.0), ["s0"], ["s1"])
+    at(-7)
+    op("V", lambda: V.memset(X("q1"), -10.0), [], ["q1"])
+    op("V", lambda: V.memset(X("q1", 15, 128, 16), -9.0), ["q1"], ["q1"])
+    iota("iy", [[16, 8], [0, 16]], early=True)
+    iota("i8", [[16, 8]], early=True)
+    vts("x128", "p16f", 128.0, None, A.mult)
+    vts("Bq", "iy", "x128", 150.0, A.add, A.add)
+    op("V", ts(X("Br"), X("s0", 0, 128), -30000.0, None, A.mult), ["s0"], ["Br"])
+    op("V", tt(X("Bc"), X("Bq"), X("Br"), A.add), ["Bq", "Br"], ["Bc"])
+    at(1)
+    vts("k16", "i8", "x128", None, A.add)
+    for n, v in (("cz", -(2.0 ** -9)), ("cr", -3 * 2.0 ** -10), ("nones", -1.0)):
+        op("V", lambda n=n, v=v: V.memset(X(n), v), [], [n])
+    iota("ik", [[16, 128]], early=True)
+    vts("ck16", "ik", "p16f", None, A.add)
+    op("S", act(X("I2"), X("I1"), scale=0.5), ["I1"], ["I2"])
+    op("S", act(X("I4"), X("I1"), scale=0.25), ["I1"], ["I4"])
+    pats = [[[128, 2], [1, 32], [32, 4]], [[128, 2], [1, 2], [2, 64]], [[128, 2], [1, 16], [16, 8]], [[1, 256]]]
+    for t in range(4):
+        at(1)
+        iota("it%d" % t, pats[t], 1024 + 256 * t)
+
+    at(1)
+    vts("i1", "p16", 3, None, A.bitwise_and)
+    vts("i2", "p16", 2, None, A.arith_shift_right)
+    vts("i3", "p16", 7, None, A.bitwise_and)
+    vts("i4", "p16", 3, None, A.arith_shift_right)
+    op("V", cp(X("f2"), X("i2")), ["i2"], ["f2"])
+    op("V", cp(X("f4"), X("i4")), ["i4"], ["f4"])
+    vts("f1", "i1", 32.0, "f2", A.mult, A.add)
+    vts("f3", "i3", 16.0, "f4", A.mult, A.add)
+    vts("g2", "p16f", 2.0, None, A.mult)
+    iota("jp", [[128, 2], [4, 8]], a=16, b=32, key="jp1")
+    iota("jp", [[128, 2], [1, 2], [32, 4]], a=32, b=48, key="jp2")
+    iota("jp", [[128, 2], [2, 8]], a=48, b=64, key="jp3")
+    for t, (k, c) in enumerate(((1, "f1"), (2, "g2"), (3, "f3"))):
+        op("V", ts(X("rb%d" % t), X("jp", 16 * k, 16 * k + 16), X(c), 32.0, A.add, A.mult), ["jp%d" % k, c], ["rb%d" % t])
+
+    def late_constants():
+        for n, d in (("Sh1", 1), ("Sh2", 2)):
+            op("G", lambda n=n, d=d: G.affine_select(X(n), X("BD"), [[1, 128]], A.is_equal, 0.0, -d, -1), ["BD"], [n])
+        for t in range(4):
+            op("V", ts(X("NF%d" % t), X("it3"), 256.0 * (t - 3), X("m0"), A.add, A.mult), ["it3", "m0"], ["NF%d" % t])
+        at(49)
+        vts("i5", "p16", 1, None, A.bitwise_and)
+        vts("i6", "p16", 1, None, A.arith_shift_right)
+        op("V", cp(X("f6"), X("i6")), ["i6"], ["f6"])
+        vts("f5", "i5", 64.0, "f6", A.mult, A.add)
+        vts("g3", "p16f", 8.0, None, A.mult)
+        iota("fr", [[0, 2], [4, 8]], a=0, b=16, key="fr")
+        iota("fr", [[0, 2], [1, 4], [64, 2]], a=16, b=32, key="fr")
+        iota("fr", [[0, 2], [8, 8]], a=32, b=48, key="fr")
+        iota("fr", [[0, 2], [1, 8]], a=48, b=64, key="fr")
+        for t, c in enumerate(("f1", "g1", "f5", "g3")):
+            op("V", ts(X("yc", 16 * t, 16 * t + 16), X("fr", 16 * t, 16 * t + 16), X(c), None, A.add), ["fr", c], ["yc"])
+        vts("yq", "yc", 3, None, A.arith_shift_right)
+        op("V", ts(X("ye", 0, 48), X("yq", 0, 48), 56.0, None, A.mult), ["yq"], ["ye"])
+        op("V", ts(X("ye", 48, 64), X("yq", 48, 64), 8.0, None, A.mult), ["yq"], ["ye"])
+        iota("yb", [[16, 4], [8, 2], [0, 8]], integer=True)
+        op("V", tt(X("yd"), X("ye"), X("yc"), A.add), ["ye", "yc"], ["yd"])
+        op("V", tt(X("yq"), X("yd"), X("yb"), A.add), ["yd", "yb"], ["yq"])
+        op("V", cp(X("yl", 0, 48), X("yq", 0, 48)), ["yq"], ["yl"])
+        op("V", ts(X("yl", 48, 64), X("yq", 48, 64), -48.0, None, A.add), ["yq"], ["yl"])
+
+    def half(h):
+        return 128 * h, 128 * h + 128
+
+    def zkey(t, h):
+        return "zr0" if t == 0 else "zr%d%d" % (t, h)
+
+    for t in (1, 2, 3):
+        src = q - 1 if t < 3 else q + 2
+        for h in range(2):
+            arrives(src, "al%d%d" % (t, h), "LR%d%d" % (t, h))
+            arrives(src, "az%d%d" % (t, h), "zr%d%d" % (t, h))
+    for t in range(4):
+        src = q + 1 + t % 3
+        if t < 3:
+            arrives(src, "ah%d" % t, "HM%d" % t)
+        else:
+            for h in range(2):
+                arrives(src, "ah3%d" % h, "HM3%d" % h)
+                arrives(src, "az4%d" % h, "zf%d" % h)
+            arrives(src, "aL3", "L3r")
+            arrives(src, "aho", "HM3o")
+
+    def Lk(t, h):
+        return "L%d%d" % (t % 2, h)
+
+    def pre_L(t, h):
+        a, b = half(h)
+        k = Lk(t, h)
+        if t == 0:
+            op("V", cp(X(k), X("L0A", a, b)), ["L0A"], [k])
+        else:
+            w = ("OB", "PC", "OA")[t - 1]
+            op("V", tt(X(k), X(w).indirect(X("LR%d" % t, 16 * h, 16 * h + 8)), X("N%d" % (t - 1), a, b), A.add),
+               [w, "LR%d%d" % (t, h), "N%d" % (t - 1)], [k])
+
+    def pre_n(t, h):
+        a, b = half(h)
+        z, zk, pu = X("zr%d" % t, a, b), zkey(t, h), "P%d" % (2 + h)
+        o = X(pu, 0, 128)
+        op("T", [mm(o, X("cu"), X("ones"), True, False)], ["cu", "ones"], [pu])
+        op("T", [mm(o, X("WB"), z, False, True)], ["WB", zk], [pu])
+        op("S", act(X("nM%d" % h), o, IDN, bias=MAGIC, scale=2.0 ** -12), [pu], ["nM%d" % h])
+        op("S", act(X("nb%d" % h), X("nM%d" % h), IDN, bias=-MAGIC), ["nM%d" % h], ["nb%d" % h])
+
+    def pre_u(t, h):
+        a, b = half(h)
+        z, zk, pu, pz = X("zr%d" % t, a, b), zkey(t, h), "P%d" % (2 + h), "P%d" % h
+        o = X(pu, 128, 256)
+        op("T", [mm(o, X("c32"), X("ones"), True, False), mm(o, X("WB"), z, False, False)], ["c32", "ones", "WB", zk], [pu])
+        op("T", [mm(o, X("I4k"), X("nb%d" % h), False, True)], ["I4k", "nb%d" % h], [pu])
+        op("T", [mm(X(pz, d, 512, 4), X("I1"), z) for d in range(4)], ["I1", zk], [pz])
+
+    def slist(t, h):
+        a, b = half(h)
+        if t < 3:
+            op("T", [mm(X("P6", 256 + 8 * h, 264 + 8 * h), X("Dw", 16 - x, 144 - x), X("zr%d" % t, a + 8 * x, a + 8 * x + 8),
+                        x == 0, x == 15) for x in range(16)], ["Dw", zkey(t, h)], ["P6"])
+
+    def pre_a(t, h):
+        pu = "P%d" % (2 + h)
+        op("V", tt(X("pr%d" % h), X(pu, 128, 256), X(Lk(t, h)), A.mult), [pu, Lk(t, h)], ["pr%d" % h])
+
+    def pre_b(t, h):
+        k = "cA" if t else "ck"
+        op("V", ts(X("aI%d" % h), X("pr%d" % h), X(k), None, A.add), ["pr%d" % h, k], ["aI%d" % h])
+        op("V", ts(X("aJ%d" % h), X("aI%d" % h), 5, 8191, A.arith_shift_right, A.bitwise_and), ["aI%d" % h], ["aJ%d" % h])
+        op("V", cp(X("al%d" % h), X("aJ%d" % h)), ["aJ%d" % h], ["al%d" % h])
+
+    def ulist(t):
+        op("V", cp(X("uI"), X("P6", 256, 272)), ["P6"], ["uI"])
+        vts("uJ", "uI", 31, None, A.bitwise_and)
+        op("V", tt(X("uK"), X("uJ"), X("rb%d" % t), A.add), ["uJ", "rb%d" % t], ["uK"])
+        op("V", cp(X("UL"), X("uK")), ["uK"], ["UL"])
+
+    def gather(t, h, j):
+        a, b = SUB[h][j], SUB[h][j + 1]
+        op("S", act(X("Y%d" % h, 16 * a, 16 * b), X("R").indirect(X("al%d" % h, a, b))), ["R", "Ra", "al%d" % h],
+           ["Y%d_%d" % (h, j)])
+
+    def compare(t, h, j, ds=(0, 1, 2, 3)):
+        a, b = 16 * SUB[h][j], 16 * SUB[h][j + 1]
+        for d in ds:
+            op("V", tt(X("B%d" % h, a + d, b, 4), X("Y%d" % h, a + d, b, 4), X("P%d" % h, a // 4, b // 4), A.is_gt),
+               ["Y%d_%d" % (h, j), "P%d" % h], ["B%d" % h])
+
+    def counts(t, h):
+        pc = "P%d" % (4 + h)
+        op("T", [mm(X(pc, 0, 128), X("Dn", 16 - x, 144 - x), X("B%d" % h, 128 * x, 128 * x + 128), x == 0, x == 15)
+                 for x in range(16)], ["Dn", "B%d" % h], [pc])
+
+    def scans(t, h):
+        yk = ["Y%d_%d" % (h, j) for j in range(len(SUB[h]) - 1)]
+        op("V", lambda: V.tensor_tensor_scan(X("HI%d" % h), X("s0"), X("Y%d" % h), 0.0, A.mult, A.max), ["s0"] + yk, ["HI%d" % h])
+        op("V", lambda: V.tensor_tensor_scan(X("LO%d" % h), X("s1"), X("Y%d" % h), 0.0, A.max, A.min), ["s1"] + yk, ["LO%d" % h])
+
+    def offs(t, h):
+        c = 16 * h + 8 if t < 3 else 16 + 8 * h
+        return X("MSG%d" % t, c, c + 8)
+
+    def lmov(t, h):
+        c = 16 * h if t < 3 else 8 * h
+        return X("MSG%d" % t, c, c + 8)
+
+    def verdict(t, h):
+        pc = "P%d" % (4 + h)
+        op("V", lambda: V.tensor_tensor_scan(X("rm%d" % h), X(pc, 0, 128), X("q1"), -9.0, A.min, A.max), [pc, "q1"], ["rm%d" % h])
+        op("V", lambda: V.tensor_tensor_scan(X("st%d" % h), X("Bc"), X("rm%d" % h), 0.0, A.max, A.add), ["Bc", "rm%d" % h],
+           ["st%d" % h])
+        op("V", cp(offs(t, h), X("st%d" % h, 14, 128, 16)), ["st%d" % h], ["of%d%d" % (t, h)])
+
+    def select(t, h, lo_on_v=False):
+        for s, w in (("hs%d" % h, "HI%d" % h), ("ls%d" % h, "LO%d" % h)):
+            i = X(w).indirect(offs(t, h))
+            if lo_on_v and s[0] == "l":
+                op("V", cp(X(s), i), [w, "of%d%d" % (t, h)], [s])
+            else:
+                op("S", act(X(s), i), [w, "of%d%d" % (t, h)], [s])
+
+    def newz_pe(t, h):
+        pu = "P%d" % (2 + h)
+        o = X(pu, 256, 384)
+        op("T", [mm(o, X("cz"), X("ones"), True, False)], ["cz", "ones"], [pu])
+        op("T", [mm(o, X("I2"), X("ls%d" % h), False, False)], ["I2", "ls%d" % h], [pu])
+        op("T", [mm(o, X("I2"), X("hs%d" % h), False, True)], ["hs%d" % h], [pu])
+
+    def rounded(h, out, in_, ki, ko):
+        if h == 0:
+            m = "rM" + ki
+            op("S", act(X(m), in_, IDN, bias=MAGIC), [ki], [m])
+            op("S", act(out, X(m), IDN, bias=-MAGIC), [m], [ko])
+        else:
+            op("V", ts(out, in_, MAGIC, MAGIC, A.add, A.subtract), [ki], [ko])
+
+    def newz(t, h):
+        a, b = half(h)
+        pu = "P%d" % (2 + h)
+        o = X(pu, 256, 384)
+        rounded(h, X("zo%d" % t, a, b), o, pu, "zo%d%d" % (t, h))
+        if t < 3:
+            send(q + 1 if t < 2 else q + 2, X("zr%d" % (t + 1), a, b), X("zo%d" % t, a, b), "az%d%d" % (t + 1, h), ["zo%d%d" % (t, h)])
+        else:
+            send(q - 1, X("zf", a, b), X("zo3", a, b), "az4%d" % h, ["zo3%d" % h])
+
+    def moves_pe(t, h):
+        pc = "P%d" % (4 + h)
+        op("T", [mm(X(pc, 128 + 8 * x, 136 + 8 * x), X("EX", 128 * x, 128 * x + 128), X("st%d" % h, 14, 128, 16)) for x in range(16)],
+           ["EX%d" % x for x in range(16)] + ["st%d" % h], [pc])
+
+    def moves_a(t, h):
+        pc = "P%d" % (4 + h)
+        op("V", tt(X(pc, 256, 384), X(pc, 128, 256), X("ck16"), A.is_equal), [pc, "ck16"], [pc])
+        op("V", tt(X("ML%d" % h), X(pc, 256, 384), X(Lk(t, h)), A.mult), [pc, Lk(t, h)], ["ML%d" % h])
+        op("T", [mm(X(pc, 384, 392), X("D16", 16 - x, 144 - x), X("ML%d" % h, 8 * x, 8 * x + 8), x == 0, x == 15)
+                 for x in range(16)], ["D16", "ML%d" % h], [pc])
+
+    def moves_b(t, h):
+        pc = "P%d" % (4 + h)
+        op("V", cp(lmov(t, h), X(pc, 384, 392)), [pc], ["lk%d%d" % (t, h)])
+        m = X("MSG%d" % t, 16 * h, 16 * h + 16)
+        ks = ["lk%d%d" % (t, h), "of%d%d" % (t, h)]
+        if t < 3:
+            send(q + 1 if t < 2 else q + 2, X("LR%d" % (t + 1), 16 * h, 16 * h + 16), m, "al%d%d" % (t + 1, h), ks)
+        else:
+            send(q - 1, X("HM3", 8 * h, 8 * h + 8), lmov(3, h), "ah3%d" % h, ks[:1])
+
+    def home_list(t):
+        send(q - 1 - t % 3, X("HM%d" % t), X("MSG%d" % t), "ah%d" % t, ["%s%d%d" % (k, t, h) for k in ("lk", "of") for h in (0, 1)])
+
+    def number_pe(t):
+        o = X("P5", 400, 408)
+        op("T", [mm(o, X("nones"), X("rm%d" % h, 14, 128, 16), h == 0, h == 1) for h in range(2)], ["nones", "rm0", "rm1"], ["P5"])
+
+    def number(t):
+        op("V", lambda: V.tensor_reduce(X("cR"), X("P5", 400, 408), AxisListType.X, A.add), ["P5"], ["cR"])
+        op("V", cp(X("cAi"), X("cR")), ["cR"], ["cAi"])
+        vts("cAj", "cAi", 255, None, A.bitwise_and)
+        vts("cA", "cAj", 32.0, "ck", A.mult, A.add)
+
+    def old(t):
+        op("S", act(X("old"), X("R").indirect(X("UL"))), ["R", "Ra", "UL"], ["old"])
+
+    def strat_pe(t, h):
+        a, b = half(h)
+        o = X("P6", a, b)
+        op("T", [mm(o, X("cr"), X("ones"), True, False), mm(o, X("I2"), X("old", a, b), False, False),
+                 mm(o, X("I4"), X("hs%d" % h), False, False), mm(o, X("I4"), X("ls%d" % h), False, True)],
+           ["cr", "ones", "I2", "I4", "old", "hs%d" % h, "ls%d" % h], ["P6"])
+
+    def strat_r(t, h):
+        a, b = half(h)
+        rounded(h, X("rn%d" % h), X("P6", a, b), "P6", "rn%d" % h)
+
+    def strat_v(t, h):
+        op("V", cp(X("R").indirect(X("UL", 8 * h, 8 * h + 8)), X("rn%d" % h)), ["rn%d" % h, "UL"], ["R"])
+
+    def table(w, r, banks=("P0", "P7")):
+        for k in range(2):
+            a, p = 512 * k, banks[k]
+            op("T", mm(X(p), X("Sh1"), X(r, a, a + 512)), ["Sh1", r], [p])
+            op("S", act(X(w, a, a + 512), X(p)), [p], [w])
+
+    def runs(t):
+        if t == 0:
+            return [((32 * b, 32 * b + 32, None), (b, 128, 4)) for b in range(4)]
+        if t == 1:
+            return [((b, 128, 4), (32 * b, 32 * b + 32, None)) for b in range(4)]
+        if t == 2:
+            return [((64 * b, 64 * b + 64, None), (b, 128, 2)) for b in range(2)]
+        return [((b, 128, 8), (16 * b, 16 * b + 16, None)) for b in range(8)]
+
+    def permuted(at, sh, Lb, t, nf, shn):
+        cs = []
+        for h in range(2):
+            for (a, b, st), (c, d, dst) in runs(t):
+                o = X("P7", at + 128 * h + c, at + 128 * h + d, dst)
+                cs.append(mm(o, X(sh), X(Lb, 128 * h + a, 128 * h + b, st), True, nf is None))
+                if nf is not None:
+                    cs.append(mm(o, X(shn), X("NF%d" % nf, 128 * h + c, 128 * h + d, dst), False, True))
+        return cs
+
+    def shifted(w, at, Lb, t, t_before, t_mover):
+        n = 0
+        cs = []
+        if t_before:
+            cs += permuted(0, "Sh1", Lb, t, None, None)
+            n = 256
+        cs += permuted(n, "Sh2", Lb, t, t_mover, "Sh1")
+        op("T", cs, ["Sh1", "Sh2", Lb, "NF%d" % t_mover], ["P7"])
+        op("S", act(X(w, at, at + n + 256), X("P7", 0, n + 256)), ["P7"], [w])
+
+    def resumed(Lb, w, lst, keys, t):
+        for h in range(2):
+            a, b = half(h)
+            op("V", tt(X(Lb, a, b), X(w).indirect(X(lst, 16 * h, 16 * h + 8)), X("N%d" % t, a, b), A.add),
+               [w, "N%d" % t] + keys, [Lb])
+
+    for t in range(4):
+        at(0 if t == 0 else 10 * t)
+        if t == 0:
+            pre_L(0, 0); pre_n(0, 0); pre_u(0, 0); pre_a(0, 0); pre_b(0, 0)
+        for j in range(len(SUB[0]) - 1):
+            gather(t, 0, j)
+        slist(t, 0)
+        if t == 2:
+            resumed("L1A", "OA", "MSG0", ["lk00", "lk01"], 0)
+        if t == 0:
+            at(2)
+            late_constants()
+            at(4)
+        compare(t, 0, 0)
+        for j in range(1, len(SUB[0]) - 1):
+            compare(t, 0, j)
+        if t == 1:
+            shifted("PC", 1024, "L0C", 0, False, 0)
+        if t == 2:
+            shifted("OA", 1024, "L1A", 1, True, 1)
+        pre_n(t, 1); slist(t, 1); pre_u(t, 1)
+        counts(t, 0)
+        pre_L(t, 1); pre_a(t, 1); pre_b(t, 1)
+        for j in range(len(SUB[1]) - 1):
+            gather(t, 1, j)
+        if t < 3:
+            ulist(t)
+            old(t)
+        if t == 0:
+            for k in range(4):
+                op("S", act(X("N%d" % k), X("it%d" % k), scale=X("m0")), ["it%d" % k, "m0"], ["N%d" % k])
+        if t == 3:
+            for h in range(2):
+                op("V", cp(X("L3h", *half(h)), X(Lk(3, h))), [Lk(3, h)], ["L3h"])
+            send(q - 1, X("L3r"), X("L3h"), "aL3", ["L3h"])
+        scans(t, 0)
+        verdict(t, 0)
+        select(t, 0)
+        moves_pe(t, 0)
+        compare(t, 1, 0, (0, 1))
+        newz_pe(t, 0)
+        moves_a(t, 0)
+        newz(t, 0)
+        if t < 3:
+            strat_pe(t, 0)
+            strat_r(t, 0)
+        if t < 2:
+            table(("OB", "PC")[t], ("rOB", "rPC")[t])
+        compare(t, 1, 0, (2, 3))
+        for j in range(1, len(SUB[1]) - 1):
+            compare(t, 1, j)
+        counts(t, 1)
+        moves_b(t, 0)
+        if t == 1:
+            table("OA", "rOA", ("P1", "P0"))
+        scans(t, 1)
+        if t < 3:
+            strat_v(t, 0)
+        verdict(t, 1)
+        if t == 3:
+            send(q - 1, X("HM3", 16, 32), X("MSG3", 16, 32), "aho", ["of30", "of31"])
+        if t < 3:
+            number_pe(t)
+            pre_n(t + 1, 0)
+            pre_u(t + 1, 0)
+        select(t, 1, True)
+        if t < 3:
+            number(t)
+            strat_pe(t, 1)
+            newz_pe(t, 1)
+            moves_pe(t, 1)
+            pre_L(t + 1, 0)
+            pre_a(t + 1, 0); pre_b(t + 1, 0)
+            strat_r(t, 1)
+            strat_v(t, 1)
+            newz(t, 1)
+            moves_a(t, 1)
+            moves_b(t, 1)
+            home_list(t)
+            if t == 0:
+                send(q + 1, X("rOA"), X("oS"), "aOA", ["oS"])
+        else:
+            moves_pe(t, 1)
+            newz_pe(t, 1)
+            newz(t, 1)
+            moves_a(t, 1)
+            moves_b(t, 1)
+
+    at(50)
+    table("SP", "pS")
+    shifted("SP", 1024, "L0h", 0, False, 0)
+    resumed("L2H", "SP", "HM1", ["HM1"], 1)
+    shifted("SP", 1280, "L2H", 2, True, 2)
+    op("T", permuted(0, "Sh1", "L3r", 3, 3, "I1"), ["Sh1", "I1", "L3r", "NF3"], ["P7"])
+    op("S", act(X("yob"), X("P7", 0, 256)), ["P7"], ["yob"])
+    dma("Y", T.yo[:, :], X("yob"), ["yob"], [])
+    for t in range(3):
+        op("V", cp(X("hk", 32 * t, 32 * t + 32), X("HM%d" % t)), ["HM%d" % t], ["hk"])
+        for h in range(2):
+            c = 32 * t + 16 * h + 8
+            op("V", tt(X("kall", 16 * t + 8 * h, 16 * t + 8 * h + 8), X("hk", c, c + 8), X("k16"), A.subtract), ["hk", "k16"], ["kall"])
+    for k in range(2):
+        op("T", [mm(X("P%d" % k, 64 * x, 64 * x + 48), X("EX", 128 * (8 * k + x), 128 * (8 * k + x) + 128), X("kall", 0, 48))
+                 for x in range(8)],
+           ["kall"] + ["EX%d" % x for x in range(16)], ["P%d" % k])
+        op("S", act(X("ykr", 512 * k, 512 * k + 512), X("P%d" % k)), ["P%d" % k], ["ykr"])
+    op("S", act(X("ykn", 0, 768), X("ykr").indirect(X("yl", 0, 48))), ["ykr", "yl"], ["ykn"])
+    dma("Y", T.yk[:, 0:768], T["ykn"][0:128:16, 0:768], ["ykn"], [])
+
+    def yp_half(h):
+        a, b = half(h)
+        op("V", tt(X("ypb", a, b), X("SP").indirect(X("HM3", 8 * h, 8 * h + 8)), X("N3", a, b), A.add),
+           ["SP", "HM3%d" % h, "N3"], ["ypb"])
+
+    yp_half(0)
+    op("V", cp(X("hk", 96, 112), X("HM3", 16, 32)), ["HM3o"], ["hk"])
+    for h in range(2):
+        op("V", tt(X("kall", 48 + 8 * h, 56 + 8 * h), X("hk", 96 + 8 * h, 104 + 8 * h), X("k16"), A.subtract), ["hk", "k16"],
+           ["kall"])
+    yp_half(1)
+    dma("Y", T.yz[:, :], X("zf"), ["zf0", "zf1"], [])
+    dma("Y", T.yp[:, :], X("ypb"), ["ypb"], [])
+    op("T", [mm(X("P2", 16 * x, 16 * x + 16), X("EX", 128 * x, 128 * x + 128), X("kall", 48, 64)) for x in range(16)],
+       ["kall"] + ["EX%d" % x for x in range(16)], ["P2"])
+    op("S", act(X("ykr3"), X("P2", 0, 256)), ["P2"], ["ykr3"])
+    op("S", act(X("ykn", 768, 1024), X("ykr3").indirect(X("yl", 48, 64))), ["ykr3", "yl"], ["ykn"])
+    dma("S", T.yk[:, 768:1024], T["ykn"][0:128:16, 768:1024], ["ykn"], [])
+    prog.sort(key=lambda e: e[:2])
+    for _, _, f, a in prog:
+        f(*a)
+    for sem, v in used.items():
+        if clock["G"].get(sem, 0) < v:
+            g.wait_ge(T.sem[sem], v)

@@ -8,7 +8,8 @@ COPY = ActivationFunctionType.Copy
 IDN = ActivationFunctionType.Identity
 MAGIC = 12582912.0
 
-SUB = {0: [0, 48, 128], 1: [0, 64, 128]}
+BC = 2
+SUB = {0: [0, 24, 72, 128], 1: [0, 64, 128]}
 
 
 def _scratch():
@@ -52,8 +53,8 @@ def _scratch():
     for n in ("pf", "p16f", "pgf", "pg16", "p1", "p2", "k15", "k14", "m0", "m1", "wf", "ck", "cA", "cR", "f1", "f2", "f3",
               "f4", "f5", "f6", "g1", "g2", "g3", "g4", "g5", "g6", "x128"):
         sb(n, 1, f)
-    sb("fr", 144, f); sb("Dn", 144, b); sb("Dw", 144, b); sb("D16", 144, h)
-    for n in ("I1", "I2", "I4", "I4k", "bda", "bdb", "BD", "WB", "cz", "cr", "cu", "c32", "ones", "nones"):
+    sb("fr", 144, f); sb("fy", 64, f); sb("Dn", 144, b); sb("Dw", 144, b); sb("D16", 144, h)
+    for n in ("I1", "I2", "I4", "I4k", "bda", "bdb", "BD", "WB", "I2e", "cr", "cu", "c32", "ones", "nones"):
         sb(n, 128, b)
     sb("ik", 128, f); sb("ck16", 128, f)
     for n in ("Sh1", "Sh2"):
@@ -232,10 +233,10 @@ def rank_program(g, core, T, topo):
     dma("Y", X("voI"), T.vo[:, :], [], ["voI"])
     at(-9)
 
-    def iota(name, pattern, base=0, cm=0, a=None, b=None, integer=False, key=None, early=False):
+    def iota(name, pattern, base=0, cm=0, a=None, b=None, integer=False, key=None, early=None):
         o = X(name, a, b)
         at0 = cur[0]
-        at(-9.5 if early else at0)
+        at(at0 if early is None else early)
         if integer:
             op("G", lambda: G.iota(o, pattern, base, cm), [], [key or name])
         else:
@@ -255,7 +256,7 @@ def rank_program(g, core, T, topo):
     send(q + 1, X("L0A"), X("L0h"), "aL0", ["L0h"])
     arrives(q - 1, "az0", "zr0"); arrives(q - 1, "aL0", "L0A")
 
-    iota("fr", [[1, 144]], -16, early=True)
+    iota("fr", [[1, 144]], -16, early=-9.5)
     vts("pg", "ip", 112, None, A.bitwise_and)
     op("V", cp(X("pf"), X("ip")), ["ip"], ["pf"])
     op("V", cp(X("p16f"), X("p16")), ["p16"], ["p16f"])
@@ -285,8 +286,6 @@ def rank_program(g, core, T, topo):
     at(-7.5)
     op("V", cp(X("pS"), X("vpI")), ["vpI"], ["pS"])
     at(2)
-    op("V", cp(X("oS"), X("voI")), ["voI"], ["oS"])
-    send(q + 2, X("rOB"), X("oS"), "aOB", ["oS"])
     send(q + 3, X("rPC"), X("pS"), "aPC", ["pS"])
     send(q + 3, X("L0C"), X("L0h"), "aL0C", ["L0h"])
     arrives(q - 2, "aOB", "rOB"); arrives(q + 1, "aPC", "rPC"); arrives(q + 1, "aL0C", "L0C"); arrives(q - 1, "aOA", "rOA")
@@ -299,19 +298,20 @@ def rank_program(g, core, T, topo):
     at(-7)
     op("V", lambda: V.memset(X("q1"), -10.0), [], ["q1"])
     op("V", lambda: V.memset(X("q1", 15, 128, 16), -9.0), ["q1"], ["q1"])
-    iota("iy", [[16, 8], [0, 16]], early=True)
-    iota("i8", [[16, 8]], early=True)
+    iota("iy", [[16, 8], [0, 16]], early=-9.5)
+    iota("i8", [[16, 8]], early=-9.5)
     vts("x128", "p16f", 128.0, None, A.mult)
     vts("Bq", "iy", "x128", 150.0, A.add, A.add)
     op("V", ts(X("Br"), X("s0", 0, 128), -30000.0, None, A.mult), ["s0"], ["Br"])
     op("V", tt(X("Bc"), X("Bq"), X("Br"), A.add), ["Bq", "Br"], ["Bc"])
     at(1)
     vts("k16", "i8", "x128", None, A.add)
-    for n, v in (("cz", -(2.0 ** -9)), ("cr", -3 * 2.0 ** -10), ("nones", -1.0)):
+    for n, v in (("cr", -3 * 2.0 ** -10), ("nones", -1.0)):
         op("V", lambda n=n, v=v: V.memset(X(n), v), [], [n])
-    iota("ik", [[16, 128]], early=True)
+    iota("ik", [[16, 128]], early=-9.5)
     vts("ck16", "ik", "p16f", None, A.add)
     op("S", act(X("I2"), X("I1"), scale=0.5), ["I1"], ["I2"])
+    op("S", act(X("I2e"), X("I1"), scale=0.5 - 2.0 ** -9), ["I1"], ["I2e"])
     op("S", act(X("I4"), X("I1"), scale=0.25), ["I1"], ["I4"])
     pats = [[[128, 2], [1, 32], [32, 4]], [[128, 2], [1, 2], [2, 64]], [[128, 2], [1, 16], [16, 8]], [[1, 256]]]
     for t in range(4):
@@ -339,22 +339,22 @@ def rank_program(g, core, T, topo):
             op("G", lambda n=n, d=d: G.affine_select(X(n), X("BD"), [[1, 128]], A.is_equal, 0.0, -d, -1), ["BD"], [n])
         for t in range(4):
             op("V", ts(X("NF%d" % t), X("it3"), 256.0 * (t - 3), X("m0"), A.add, A.mult), ["it3", "m0"], ["NF%d" % t])
-        at(49)
+
+    for k, pat in enumerate(([[0, 2], [4, 8]], [[0, 2], [1, 4], [64, 2]], [[0, 2], [8, 8]], [[0, 2], [1, 8]])):
+        iota("fy", pat, a=16 * k, b=16 * k + 16, key="fy%d" % k, early=2.5)
+    iota("yb", [[16, 4], [8, 2], [0, 8]], integer=True, early=2.5)
+
+    def list_constants():
         vts("i5", "p16", 1, None, A.bitwise_and)
         vts("i6", "p16", 1, None, A.arith_shift_right)
         op("V", cp(X("f6"), X("i6")), ["i6"], ["f6"])
         vts("f5", "i5", 64.0, "f6", A.mult, A.add)
         vts("g3", "p16f", 8.0, None, A.mult)
-        iota("fr", [[0, 2], [4, 8]], a=0, b=16, key="fr")
-        iota("fr", [[0, 2], [1, 4], [64, 2]], a=16, b=32, key="fr")
-        iota("fr", [[0, 2], [8, 8]], a=32, b=48, key="fr")
-        iota("fr", [[0, 2], [1, 8]], a=48, b=64, key="fr")
         for t, c in enumerate(("f1", "g1", "f5", "g3")):
-            op("V", ts(X("yc", 16 * t, 16 * t + 16), X("fr", 16 * t, 16 * t + 16), X(c), None, A.add), ["fr", c], ["yc"])
+            op("V", ts(X("yc", 16 * t, 16 * t + 16), X("fy", 16 * t, 16 * t + 16), X(c), None, A.add), ["fy%d" % t, c], ["yc"])
         vts("yq", "yc", 3, None, A.arith_shift_right)
         op("V", ts(X("ye", 0, 48), X("yq", 0, 48), 56.0, None, A.mult), ["yq"], ["ye"])
         op("V", ts(X("ye", 48, 64), X("yq", 48, 64), 8.0, None, A.mult), ["yq"], ["ye"])
-        iota("yb", [[16, 4], [8, 2], [0, 8]], integer=True)
         op("V", tt(X("yd"), X("ye"), X("yc"), A.add), ["ye", "yc"], ["yd"])
         op("V", tt(X("yq"), X("yd"), X("yb"), A.add), ["yd", "yb"], ["yq"])
         op("V", cp(X("yl", 0, 48), X("yq", 0, 48)), ["yq"], ["yl"])
@@ -436,23 +436,31 @@ def rank_program(g, core, T, topo):
 
     def gather(t, h, j):
         a, b = SUB[h][j], SUB[h][j + 1]
-        op("S", act(X("Y%d" % h, 16 * a, 16 * b), X("R").indirect(X("al%d" % h, a, b))), ["R", "Ra", "al%d" % h],
-           ["Y%d_%d" % (h, j)])
+        o, i = X("Y%d" % h, 16 * a, 16 * b), X("R").indirect(X("al%d" % h, a, b))
+        v = h == 0 and j == 0
+        op("V" if v else "S", cp(o, i) if v else act(o, i), ["R", "Ra", "al%d" % h], ["Y%d_%d" % (h, j)])
 
     def compare(t, h, j, ds=(0, 1, 2, 3)):
         a, b = 16 * SUB[h][j], 16 * SUB[h][j + 1]
         for d in ds:
             op("V", tt(X("B%d" % h, a + d, b, 4), X("Y%d" % h, a + d, b, 4), X("P%d" % h, a // 4, b // 4), A.is_gt),
-               ["Y%d_%d" % (h, j), "P%d" % h], ["B%d" % h])
+               ["Y%d_%d" % (h, j), "P%d" % h], ["B%d_%d" % (h, j)])
 
-    def counts(t, h):
+    def counts(t, h, j):
         pc = "P%d" % (4 + h)
         op("T", [mm(X(pc, 0, 128), X("Dn", 16 - x, 144 - x), X("B%d" % h, 128 * x, 128 * x + 128), x == 0, x == 15)
-                 for x in range(16)], ["Dn", "B%d" % h], [pc])
+                 for x in range(SUB[h][j] // 8, SUB[h][j + 1] // 8)], ["Dn", "B%d_%d" % (h, j)], [pc])
 
     def scans(t, h):
+        scan_hi(t, h)
+        scan_lo(t, h)
+
+    def scan_hi(t, h):
         yk = ["Y%d_%d" % (h, j) for j in range(len(SUB[h]) - 1)]
         op("V", lambda: V.tensor_tensor_scan(X("HI%d" % h), X("s0"), X("Y%d" % h), 0.0, A.mult, A.max), ["s0"] + yk, ["HI%d" % h])
+
+    def scan_lo(t, h):
+        yk = ["Y%d_%d" % (h, j) for j in range(len(SUB[h]) - 1)]
         op("V", lambda: V.tensor_tensor_scan(X("LO%d" % h), X("s1"), X("Y%d" % h), 0.0, A.max, A.min), ["s1"] + yk, ["LO%d" % h])
 
     def offs(t, h):
@@ -481,9 +489,8 @@ def rank_program(g, core, T, topo):
     def newz_pe(t, h):
         pu = "P%d" % (2 + h)
         o = X(pu, 256, 384)
-        op("T", [mm(o, X("cz"), X("ones"), True, False)], ["cz", "ones"], [pu])
-        op("T", [mm(o, X("I2"), X("ls%d" % h), False, False)], ["I2", "ls%d" % h], [pu])
-        op("T", [mm(o, X("I2"), X("hs%d" % h), False, True)], ["hs%d" % h], [pu])
+        op("T", [mm(o, X("I2"), X("ls%d" % h), True, False)], ["I2", "ls%d" % h], [pu])
+        op("T", [mm(o, X("I2e"), X("hs%d" % h), False, True)], ["I2e", "hs%d" % h], [pu])
 
     def rounded(h, out, in_, ki, ko):
         if h == 0:
@@ -503,10 +510,10 @@ def rank_program(g, core, T, topo):
         else:
             send(q - 1, X("zf", a, b), X("zo3", a, b), "az4%d" % h, ["zo3%d" % h])
 
-    def moves_pe(t, h):
+    def moves_pe(t, h, a=0, b=16):
         pc = "P%d" % (4 + h)
-        op("T", [mm(X(pc, 128 + 8 * x, 136 + 8 * x), X("EX", 128 * x, 128 * x + 128), X("st%d" % h, 14, 128, 16)) for x in range(16)],
-           ["EX%d" % x for x in range(16)] + ["st%d" % h], [pc])
+        op("T", [mm(X(pc, 128 + 8 * x, 136 + 8 * x), X("EX", 128 * x, 128 * x + 128), X("st%d" % h, 14, 128, 16)) for x in range(a, b)],
+           ["EX%d" % x for x in range(a, b)] + ["st%d" % h], [pc])
 
     def moves_a(t, h):
         pc = "P%d" % (4 + h)
@@ -544,9 +551,14 @@ def rank_program(g, core, T, topo):
     def strat_pe(t, h):
         a, b = half(h)
         o = X("P6", a, b)
-        op("T", [mm(o, X("cr"), X("ones"), True, False), mm(o, X("I2"), X("old", a, b), False, False),
-                 mm(o, X("I4"), X("hs%d" % h), False, False), mm(o, X("I4"), X("ls%d" % h), False, True)],
-           ["cr", "ones", "I2", "I4", "old", "hs%d" % h, "ls%d" % h], ["P6"])
+        op("T", [mm(o, X("I4"), X("ls%d" % h), False, False), mm(o, X("I4"), X("hs%d" % h), False, True)],
+           ["I4", "hs%d" % h, "ls%d" % h], ["P6"])
+
+    def strat_pre(t, h):
+        a, b = half(h)
+        o = X("P6", a, b)
+        op("T", [mm(o, X("cr"), X("ones"), True, False), mm(o, X("I2"), X("old", a, b), False, False)],
+           ["cr", "ones", "I2", "old"], ["P6"])
 
     def strat_r(t, h):
         a, b = half(h)
@@ -575,10 +587,11 @@ def rank_program(g, core, T, topo):
         for h in range(2):
             for (a, b, st), (c, d, dst) in runs(t):
                 o = X("P7", at + 128 * h + c, at + 128 * h + d, dst)
-                cs.append(mm(o, X(sh), X(Lb, 128 * h + a, 128 * h + b, st), True, nf is None))
-                if nf is not None:
-                    cs.append(mm(o, X(shn), X("NF%d" % nf, 128 * h + c, 128 * h + d, dst), False, True))
-        return cs
+                cs.append((o, X(sh), X(Lb, 128 * h + a, 128 * h + b, st)))
+        if nf is None:
+            return [mm(*c) for c in cs]
+        return [mm(X("P7", at, at + 256), X(shn), X("NF%d" % nf), True, False)] + [
+            mm(*c, False, c is cs[-1]) for c in cs]
 
     def shifted(w, at, Lb, t, t_before, t_mover):
         n = 0
@@ -600,57 +613,72 @@ def rank_program(g, core, T, topo):
         at(0 if t == 0 else 10 * t)
         if t == 0:
             pre_L(0, 0); pre_n(0, 0); pre_u(0, 0); pre_a(0, 0); pre_b(0, 0)
-        for j in range(len(SUB[0]) - 1):
+        for j in range(1 if t else 0, len(SUB[0]) - 1):
             gather(t, 0, j)
         slist(t, 0)
-        if t == 2:
-            resumed("L1A", "OA", "MSG0", ["lk00", "lk01"], 0)
         if t == 0:
             at(2)
             late_constants()
             at(4)
-        compare(t, 0, 0)
+        if t == 0:
+            compare(t, 0, 0)
+            counts(t, 0, 0)
+        if t:
+            table(("PC", "OA", "SP")[t - 1], ("rPC", "rOA", "pS")[t - 1], ("P7", "P5"))
         for j in range(1, len(SUB[0]) - 1):
             compare(t, 0, j)
-        if t == 1:
-            shifted("PC", 1024, "L0C", 0, False, 0)
-        if t == 2:
-            shifted("OA", 1024, "L1A", 1, True, 1)
-        pre_n(t, 1); slist(t, 1); pre_u(t, 1)
-        counts(t, 0)
+            if j == len(SUB[0]) - 2:
+                pre_n(t, 1)
+                pre_u(t, 1)
+            counts(t, 0, j)
+        slist(t, 1)
+        if t:
+            scan_hi(t, 0)
         pre_L(t, 1); pre_a(t, 1); pre_b(t, 1)
         for j in range(len(SUB[1]) - 1):
             gather(t, 1, j)
-        if t < 3:
-            ulist(t)
-            old(t)
+        if t == 1:
+            shifted("PC", 1024, "L0C", 0, False, 0)
+        if t == 2:
+            resumed("L1A", "OA", "MSG0", ["lk00", "lk01"], 0)
+            shifted("OA", 1024, "L1A", 1, True, 1)
+        if t == 3:
+            shifted("SP", 1024, "L0h", 0, False, 0)
         if t == 0:
+            op("V", cp(X("oS"), X("voI")), ["voI"], ["oS"])
+            send(q + 2, X("rOB"), X("oS"), "aOB", ["oS"])
             for k in range(4):
                 op("S", act(X("N%d" % k), X("it%d" % k), scale=X("m0")), ["it%d" % k, "m0"], ["N%d" % k])
         if t == 3:
             for h in range(2):
                 op("V", cp(X("L3h", *half(h)), X(Lk(3, h))), [Lk(3, h)], ["L3h"])
             send(q - 1, X("L3r"), X("L3h"), "aL3", ["L3h"])
-        scans(t, 0)
+        if t == 0:
+            scan_hi(t, 0)
+        scan_lo(t, 0)
         verdict(t, 0)
         select(t, 0)
+        if t < 3:
+            ulist(t)
+            old(t)
         moves_pe(t, 0)
-        compare(t, 1, 0, (0, 1))
-        newz_pe(t, 0)
+        compare(t, 1, 0)
         moves_a(t, 0)
+        newz_pe(t, 0)
         newz(t, 0)
         if t < 3:
+            strat_pre(t, 0)
             strat_pe(t, 0)
             strat_r(t, 0)
-        if t < 2:
-            table(("OB", "PC")[t], ("rOB", "rPC")[t])
-        compare(t, 1, 0, (2, 3))
+        counts(t, 1, 0)
         for j in range(1, len(SUB[1]) - 1):
             compare(t, 1, j)
-        counts(t, 1)
+            counts(t, 1, j)
         moves_b(t, 0)
-        if t == 1:
-            table("OA", "rOA", ("P1", "P0"))
+        if t < 3:
+            strat_pre(t, 1)
+        if t == 0:
+            table("OB", "rOB", ("P1", "P7"))
         scans(t, 1)
         if t < 3:
             strat_v(t, 0)
@@ -660,19 +688,23 @@ def rank_program(g, core, T, topo):
         if t < 3:
             number_pe(t)
             pre_n(t + 1, 0)
-            pre_u(t + 1, 0)
         select(t, 1, True)
         if t < 3:
             number(t)
+            moves_pe(t, 1, 0, BC)
+            pre_u(t + 1, 0)
             strat_pe(t, 1)
             newz_pe(t, 1)
-            moves_pe(t, 1)
+            moves_pe(t, 1, BC, 16)
             pre_L(t + 1, 0)
             pre_a(t + 1, 0); pre_b(t + 1, 0)
             strat_r(t, 1)
             strat_v(t, 1)
             newz(t, 1)
+            gather(t + 1, 0, 0)
             moves_a(t, 1)
+            compare(t + 1, 0, 0)
+            counts(t + 1, 0, 0)
             moves_b(t, 1)
             home_list(t)
             if t == 0:
@@ -680,30 +712,29 @@ def rank_program(g, core, T, topo):
         else:
             moves_pe(t, 1)
             newz_pe(t, 1)
+            for k in range(3):
+                op("V", cp(X("hk", 32 * k, 32 * k + 32), X("HM%d" % k)), ["HM%d" % k], ["hk%d" % k])
+                for h in range(2):
+                    c = 32 * k + 16 * h + 8
+                    op("V", tt(X("kall", 16 * k + 8 * h, 16 * k + 8 * h + 8), X("hk", c, c + 8), X("k16"), A.subtract),
+                       ["hk%d" % k, "k16"], ["kall"])
             newz(t, 1)
             moves_a(t, 1)
+            resumed("L2H", "SP", "HM1", ["HM1"], 1)
+            shifted("SP", 1280, "L2H", 2, True, 2)
             moves_b(t, 1)
+            list_constants()
 
     at(50)
-    table("SP", "pS")
-    shifted("SP", 1024, "L0h", 0, False, 0)
-    resumed("L2H", "SP", "HM1", ["HM1"], 1)
-    shifted("SP", 1280, "L2H", 2, True, 2)
     op("T", permuted(0, "Sh1", "L3r", 3, 3, "I1"), ["Sh1", "I1", "L3r", "NF3"], ["P7"])
     op("S", act(X("yob"), X("P7", 0, 256)), ["P7"], ["yob"])
     dma("Y", T.yo[:, :], X("yob"), ["yob"], [])
-    for t in range(3):
-        op("V", cp(X("hk", 32 * t, 32 * t + 32), X("HM%d" % t)), ["HM%d" % t], ["hk"])
-        for h in range(2):
-            c = 32 * t + 16 * h + 8
-            op("V", tt(X("kall", 16 * t + 8 * h, 16 * t + 8 * h + 8), X("hk", c, c + 8), X("k16"), A.subtract), ["hk", "k16"], ["kall"])
     for k in range(2):
         op("T", [mm(X("P%d" % k, 64 * x, 64 * x + 48), X("EX", 128 * (8 * k + x), 128 * (8 * k + x) + 128), X("kall", 0, 48))
                  for x in range(8)],
            ["kall"] + ["EX%d" % x for x in range(16)], ["P%d" % k])
         op("S", act(X("ykr", 512 * k, 512 * k + 512), X("P%d" % k)), ["P%d" % k], ["ykr"])
     op("S", act(X("ykn", 0, 768), X("ykr").indirect(X("yl", 0, 48))), ["ykr", "yl"], ["ykn"])
-    dma("Y", T.yk[:, 0:768], T["ykn"][0:128:16, 0:768], ["ykn"], [])
 
     def yp_half(h):
         a, b = half(h)
@@ -711,18 +742,18 @@ def rank_program(g, core, T, topo):
            ["SP", "HM3%d" % h, "N3"], ["ypb"])
 
     yp_half(0)
-    op("V", cp(X("hk", 96, 112), X("HM3", 16, 32)), ["HM3o"], ["hk"])
+    op("V", cp(X("hk", 96, 112), X("HM3", 16, 32)), ["HM3o"], ["hk3"])
     for h in range(2):
-        op("V", tt(X("kall", 48 + 8 * h, 56 + 8 * h), X("hk", 96 + 8 * h, 104 + 8 * h), X("k16"), A.subtract), ["hk", "k16"],
-           ["kall"])
+        op("V", tt(X("kall", 48 + 8 * h, 56 + 8 * h), X("hk", 96 + 8 * h, 104 + 8 * h), X("k16"), A.subtract), ["hk3", "k16"],
+           ["kal3"])
     yp_half(1)
     dma("Y", T.yz[:, :], X("zf"), ["zf0", "zf1"], [])
     dma("Y", T.yp[:, :], X("ypb"), ["ypb"], [])
     op("T", [mm(X("P2", 16 * x, 16 * x + 16), X("EX", 128 * x, 128 * x + 128), X("kall", 48, 64)) for x in range(16)],
-       ["kall"] + ["EX%d" % x for x in range(16)], ["P2"])
+       ["kal3"] + ["EX%d" % x for x in range(16)], ["P2"])
     op("S", act(X("ykr3"), X("P2", 0, 256)), ["P2"], ["ykr3"])
     op("S", act(X("ykn", 768, 1024), X("ykr3").indirect(X("yl", 48, 64))), ["ykr3", "yl"], ["ykn"])
-    dma("S", T.yk[:, 768:1024], T["ykn"][0:128:16, 768:1024], ["ykn"], [])
+    dma("S", T.yk[:, :], T["ykn"][0:128:16, :], ["ykn"], [])
     prog.sort(key=lambda e: e[:2])
     for _, _, f, a in prog:
         f(*a)

@@ -9,7 +9,7 @@ IDN = ActivationFunctionType.Identity
 MAGIC = 12582912.0
 
 BC = 2
-SUB = {0: [0, 24, 72, 128], 1: [0, 64, 128]}
+SUB = {0: [0, 8, 72, 128], 1: [0, 72, 128]}
 
 
 def _scratch():
@@ -29,12 +29,13 @@ def _scratch():
             sb("L%d%d" % (p, k), 128, f)
     for t in range(4):
         sb("MSG%d" % t, 32, u); sb("zo%d" % t, 256, b); sb("zr%d" % t, 256, b); sb("HM%d" % t, 32, u)
-        sb("it%d" % t, 256, f); sb("N%d" % t, 256, f); sb("NF%d" % t, 256, h)
+        sb("it%d" % t, 256, f); sb("N%d" % t, 256, f); sb("Hi%d" % t, 256, b)
         if t:
             sb("LR%d" % t, 32, u)
         if t < 3:
             sb("rb%d" % t, 16, i)
-    sb("zf", 256, b); sb("rMP2", 128, f); sb("rMP6", 128, f)
+    sb("Lo", 256, b); sb("e0", 256, b); sb("il", 256, f)
+    sb("zf", 256, b); sb("rM", 128, f)
     for n in ("uI", "uJ", "uK"):
         sb(n, 16, i)
     sb("UL", 16, u); sb("old", 256, b)
@@ -53,7 +54,7 @@ def _scratch():
     for n in ("pf", "p16f", "pgf", "pg16", "p1", "p2", "k15", "k14", "m0", "m1", "wf", "ck", "cA", "cR", "f1", "f2", "f3",
               "f4", "f5", "f6", "g1", "g2", "g3", "g4", "g5", "g6", "x128"):
         sb(n, 1, f)
-    sb("fr", 144, f); sb("fy", 64, f); sb("Dn", 144, b); sb("Dw", 144, b); sb("D16", 144, h)
+    sb("fr", 144, f); sb("fy", 64, f); sb("Dn", 144, b); sb("Dw", 144, b); sb("D16", 144, b)
     for n in ("I1", "I2", "I4", "I4k", "bda", "bdb", "BD", "WB", "I2e", "cr", "cu", "c32", "ones", "nones"):
         sb(n, 128, b)
     sb("ik", 128, f); sb("ck16", 128, f)
@@ -64,7 +65,7 @@ def _scratch():
     sb("jp", 96, f)
     sb("pl", 16, u); sb("yc", 64, i); sb("yq", 64, i); sb("ye", 64, i); sb("yb", 64, i); sb("yd", 64, i); sb("yl", 64, u)
     sb("hk", 128, f); sb("kall", 64, b)
-    sb("ykr", 1024, f); sb("ykr3", 256, f); sb("ykn", 1024, f); sb("ypb", 256, f); sb("yob", 256, f)
+    sb("ykr", 768, f); sb("ykr3", 256, f); sb("ykn", 1024, f); sb("ypb", 256, f); sb("yob", 256, f)
     return s
 
 
@@ -249,9 +250,9 @@ def rank_program(g, core, T, topo):
     vts("g1", "p16", 4.0, None, A.mult)
     op("V", cp(X("mvu"), X("mvI")), ["mvI"], ["mvu"])
     op("V", ts(X("pl"), X("jp", 0, 16), X("g1"), None, A.add), ["jp0", "g1"], ["pl"])
-    op("S", act(X("zs"), X("zn").indirect(X("pl"))), ["zn", "pl"], ["zs"])
     op("V", cp(X("L0n"), X("vpI").indirect(X("mvu"))), ["vpI", "mvu"], ["L0n"])
     op("V", cp(X("L0h"), X("L0n").indirect(X("pl"))), ["L0n", "pl"], ["L0h"])
+    op("S", act(X("zs"), X("zn").indirect(X("pl"))), ["zn", "pl"], ["zs"])
     send(q + 1, X("zr0"), X("zs"), "az0", ["zs"])
     send(q + 1, X("L0A"), X("L0h"), "aL0", ["L0h"])
     arrives(q - 1, "az0", "zr0"); arrives(q - 1, "aL0", "L0A")
@@ -262,24 +263,23 @@ def rank_program(g, core, T, topo):
     op("V", cp(X("p16f"), X("p16")), ["p16"], ["p16f"])
     op("V", cp(X("pgf"), X("pg")), ["pg"], ["pgf"])
     op("V", cp(X("wf"), X("wI")), ["wI"], ["wf"])
+    op("V", ts(X("I1"), X("fr", 16, 144), X("pf"), None, A.is_equal), ["fr", "pf"], ["I1"])
     vts("pg16", "pgf", 16.0, None, A.add)
-    vts("m1", "p16f", 0.0, None, A.is_gt)
     vts("m0", "p16f", 0.0, None, A.is_equal)
     vts("ck", "p16f", 1184.0, None, A.mult)
     fr = X("fr", 16, 144)
     op("V", ts(X("bda"), fr, X("pgf"), None, A.is_ge), ["fr", "pgf"], ["bda"])
     op("V", ts(X("bdb"), fr, X("pg16"), None, A.is_lt), ["fr", "pg16"], ["bdb"])
     op("V", tt(X("BD"), X("bda"), X("bdb"), A.mult), ["bda", "bdb"], ["BD"])
-    vts("WB", "BD", "wf", None, A.mult)
-    op("V", ts(X("I4k"), fr, X("pf"), -4096.0, A.is_equal, A.mult), ["fr", "pf"], ["I4k"])
+    op("S", act(X("WB"), X("BD"), scale=X("wf")), ["BD", "wf"], ["WB"])
+    op("S", act(X("I4k"), X("I1"), scale=-4096.0), ["I1"], ["I4k"])
     op("V", lambda: V.memset(X("cu", rows=slice(0, 64)), -32.0), [], ["cu"])
     op("V", lambda: V.memset(X("cu", rows=slice(64, 128)), 2.0 ** -7), [], ["cu"])
     for n, v in (("ones", 1.0), ("c32", 0.25)):
         op("V", lambda n=n, v=v: V.memset(X(n), v), [], [n])
-    op("V", ts(X("I1"), fr, X("pf"), None, A.is_equal), ["fr", "pf"], ["I1"])
-    op("V", ts(X("Dw"), X("fr"), X("pgf"), X("wf"), A.is_equal, A.mult), ["fr", "pgf", "wf"], ["Dw"])
-    op("V", ts(X("Dn"), X("fr"), X("pgf"), -1.0, A.is_equal, A.mult), ["fr", "pgf"], ["Dn"])
     op("V", ts(X("D16"), X("fr"), X("pgf"), None, A.is_equal), ["fr", "pgf"], ["D16"])
+    op("S", act(X("Dw"), X("D16"), scale=X("wf")), ["D16", "wf"], ["Dw"])
+    op("S", act(X("Dn"), X("D16"), scale=-1.0), ["D16"], ["Dn"])
     op("V", ts(X("ind"), X("fr", 16, 32), X("p16f"), None, A.is_equal), ["fr", "p16f"], ["ind"])
     for x in range(16):
         op("S", act(X("EX", 128 * x, 128 * x + 128), X("BD"), scale=X("ind", x, x + 1)), ["BD", "ind"], ["EX%d" % x])
@@ -309,7 +309,8 @@ def rank_program(g, core, T, topo):
     for n, v in (("cr", -3 * 2.0 ** -10), ("nones", -1.0)):
         op("V", lambda n=n, v=v: V.memset(X(n), v), [], [n])
     iota("ik", [[16, 128]], early=-9.5)
-    vts("ck16", "ik", "p16f", None, A.add)
+    op("S", act(X("ck16"), X("ik"), IDN, bias=X("p16f")), ["ik", "p16f"], ["ck16"])
+    at(-7)
     op("S", act(X("I2"), X("I1"), scale=0.5), ["I1"], ["I2"])
     op("S", act(X("I2e"), X("I1"), scale=0.5 - 2.0 ** -9), ["I1"], ["I2e"])
     op("S", act(X("I4"), X("I1"), scale=0.25), ["I1"], ["I4"])
@@ -337,23 +338,41 @@ def rank_program(g, core, T, topo):
     def late_constants():
         for n, d in (("Sh1", 1), ("Sh2", 2)):
             op("G", lambda n=n, d=d: G.affine_select(X(n), X("BD"), [[1, 128]], A.is_equal, 0.0, -d, -1), ["BD"], [n])
-        for t in range(4):
-            op("V", ts(X("NF%d" % t), X("it3"), 256.0 * (t - 3), X("m0"), A.add, A.mult), ["it3", "m0"], ["NF%d" % t])
+        iota("il", [[1, 256]])
+
+    def number_n(k):
+        op("S", act(X("N%d" % k), X("it%d" % k), scale=X("m0")), ["it%d" % k, "m0"], ["N%d" % k])
+
+    def number_lo():
+        op("S", act(X("Lo"), X("il"), scale=X("m0")), ["il", "m0"], ["Lo"])
+        op("S", act(X("e0"), X("il"), IDN, scale=0.0, bias=X("m0")), ["il", "m0"], ["e0"])
+
+    def number_hi(k):
+        op("S", act(X("Hi%d" % k), X("e0"), scale=1024.0 + 256 * k), ["e0"], ["Hi%d" % k])
 
     for k, pat in enumerate(([[0, 2], [4, 8]], [[0, 2], [1, 4], [64, 2]], [[0, 2], [8, 8]], [[0, 2], [1, 8]])):
         iota("fy", pat, a=16 * k, b=16 * k + 16, key="fy%d" % k, early=2.5)
     iota("yb", [[16, 4], [8, 2], [0, 8]], integer=True, early=2.5)
 
-    def list_constants():
-        vts("i5", "p16", 1, None, A.bitwise_and)
-        vts("i6", "p16", 1, None, A.arith_shift_right)
-        op("V", cp(X("f6"), X("i6")), ["i6"], ["f6"])
-        vts("f5", "i5", 64.0, "f6", A.mult, A.add)
-        vts("g3", "p16f", 8.0, None, A.mult)
+    def verdicts_home(k):
+        op("V", cp(X("hk", 32 * k, 32 * k + 32), X("HM%d" % k)), ["HM%d" % k], ["hk%d" % k])
+        for h in range(2):
+            c = 32 * k + 16 * h + 8
+            op("V", tt(X("kall", 16 * k + 8 * h, 16 * k + 8 * h + 8), X("hk", c, c + 8), X("k16"), A.subtract),
+               ["hk%d" % k, "k16"], ["kall"])
+
+    def list_constants(part):
+        if part == 0:
+            vts("i5", "p16", 1, None, A.bitwise_and)
+            vts("i6", "p16", 1, None, A.arith_shift_right)
+            op("V", cp(X("f6"), X("i6")), ["i6"], ["f6"])
+            vts("f5", "i5", 64.0, "f6", A.mult, A.add)
+            vts("g3", "p16f", 8.0, None, A.mult)
+            return
         for t, c in enumerate(("f1", "g1", "f5", "g3")):
             op("V", ts(X("yc", 16 * t, 16 * t + 16), X("fy", 16 * t, 16 * t + 16), X(c), None, A.add), ["fy%d" % t, c], ["yc"])
         vts("yq", "yc", 3, None, A.arith_shift_right)
-        op("V", ts(X("ye", 0, 48), X("yq", 0, 48), 56.0, None, A.mult), ["yq"], ["ye"])
+        op("V", ts(X("ye", 0, 48), X("yq", 0, 48), 40.0, None, A.mult), ["yq"], ["ye"])
         op("V", ts(X("ye", 48, 64), X("yq", 48, 64), 8.0, None, A.mult), ["yq"], ["ye"])
         op("V", tt(X("yd"), X("ye"), X("yc"), A.add), ["ye", "yc"], ["yd"])
         op("V", tt(X("yq"), X("yd"), X("yb"), A.add), ["yd", "yb"], ["yq"])
@@ -406,11 +425,14 @@ def rank_program(g, core, T, topo):
 
     def pre_u(t, h):
         a, b = half(h)
-        z, zk, pu, pz = X("zr%d" % t, a, b), zkey(t, h), "P%d" % (2 + h), "P%d" % h
+        z, zk, pu = X("zr%d" % t, a, b), zkey(t, h), "P%d" % (2 + h)
         o = X(pu, 128, 256)
         op("T", [mm(o, X("c32"), X("ones"), True, False), mm(o, X("WB"), z, False, False)], ["c32", "ones", "WB", zk], [pu])
         op("T", [mm(o, X("I4k"), X("nb%d" % h), False, True)], ["I4k", "nb%d" % h], [pu])
-        op("T", [mm(X(pz, d, 512, 4), X("I1"), z) for d in range(4)], ["I1", zk], [pz])
+
+    def pre_z(t, h):
+        a, b = half(h)
+        op("T", [mm(X("P%d" % h, d, 512, 4), X("I1"), X("zr%d" % t, a, b)) for d in range(4)], ["I1", zkey(t, h)], ["P%d" % h])
 
     def slist(t, h):
         a, b = half(h)
@@ -493,8 +515,8 @@ def rank_program(g, core, T, topo):
         op("T", [mm(o, X("I2e"), X("hs%d" % h), False, True)], ["I2e", "hs%d" % h], [pu])
 
     def rounded(h, out, in_, ki, ko):
-        if h == 0:
-            m = "rM" + ki
+        if ko == "rn0":
+            m = "rM"
             op("S", act(X(m), in_, IDN, bias=MAGIC), [ki], [m])
             op("S", act(out, X(m), IDN, bias=-MAGIC), [m], [ko])
         else:
@@ -515,12 +537,20 @@ def rank_program(g, core, T, topo):
         op("T", [mm(X(pc, 128 + 8 * x, 136 + 8 * x), X("EX", 128 * x, 128 * x + 128), X("st%d" % h, 14, 128, 16)) for x in range(a, b)],
            ["EX%d" % x for x in range(a, b)] + ["st%d" % h], [pc])
 
-    def moves_a(t, h):
+    def moves_v(t, h, a=0, b=16):
         pc = "P%d" % (4 + h)
-        op("V", tt(X(pc, 256, 384), X(pc, 128, 256), X("ck16"), A.is_equal), [pc, "ck16"], [pc])
-        op("V", tt(X("ML%d" % h), X(pc, 256, 384), X(Lk(t, h)), A.mult), [pc, Lk(t, h)], ["ML%d" % h])
+        a, b = 8 * a, 8 * b
+        op("V", tt(X(pc, 256 + a, 256 + b), X(pc, 128 + a, 128 + b), X("ck16", a, b), A.is_equal), [pc, "ck16"], [pc])
+        op("V", tt(X("ML%d" % h, a, b), X(pc, 256 + a, 256 + b), X(Lk(t, h), a, b), A.mult), [pc, Lk(t, h)], ["ML%d_%d" % (h, a)])
+
+    def moves_f(t, h, a=0, b=16):
+        pc = "P%d" % (4 + h)
         op("T", [mm(X(pc, 384, 392), X("D16", 16 - x, 144 - x), X("ML%d" % h, 8 * x, 8 * x + 8), x == 0, x == 15)
-                 for x in range(16)], ["D16", "ML%d" % h], [pc])
+                 for x in range(a, b)], ["D16", "ML%d_%d" % (h, 8 * a)], [pc])
+
+    def moves_a(t, h):
+        moves_v(t, h)
+        moves_f(t, h)
 
     def moves_b(t, h):
         pc = "P%d" % (4 + h)
@@ -590,18 +620,26 @@ def rank_program(g, core, T, topo):
                 cs.append((o, X(sh), X(Lb, 128 * h + a, 128 * h + b, st)))
         if nf is None:
             return [mm(*c) for c in cs]
-        return [mm(X("P7", at, at + 256), X(shn), X("NF%d" % nf), True, False)] + [
+        o = X("P7", at, at + 256)
+        return [mm(o, X(shn), X("Lo"), True, False), mm(o, X(shn), X("Hi%d" % nf), False, False)] + [
             mm(*c, False, c is cs[-1]) for c in cs]
 
     def shifted(w, at, Lb, t, t_before, t_mover):
+        shifted_pe(Lb, t, t_before, t_mover)
+        shifted_act(w, at, t_before)
+
+    def shifted_act(w, at, t_before):
+        n = 512 if t_before else 256
+        op("S", act(X(w, at, at + n), X("P7", 0, n)), ["P7"], [w])
+
+    def shifted_pe(Lb, t, t_before, t_mover):
         n = 0
         cs = []
         if t_before:
             cs += permuted(0, "Sh1", Lb, t, None, None)
             n = 256
         cs += permuted(n, "Sh2", Lb, t, t_mover, "Sh1")
-        op("T", cs, ["Sh1", "Sh2", Lb, "NF%d" % t_mover], ["P7"])
-        op("S", act(X(w, at, at + n + 256), X("P7", 0, n + 256)), ["P7"], [w])
+        op("T", cs, ["Sh1", "Sh2", Lb, "Lo", "Hi%d" % t_mover], ["P7"])
 
     def resumed(Lb, w, lst, keys, t):
         for h in range(2):
@@ -612,43 +650,47 @@ def rank_program(g, core, T, topo):
     for t in range(4):
         at(0 if t == 0 else 10 * t)
         if t == 0:
-            pre_L(0, 0); pre_n(0, 0); pre_u(0, 0); pre_a(0, 0); pre_b(0, 0)
-        for j in range(1 if t else 0, len(SUB[0]) - 1):
+            pre_L(0, 0); pre_n(0, 0); pre_n(0, 1)
+            for h in range(2):
+                if h:
+                    pre_L(0, 1)
+                pre_u(0, h); pre_z(0, h); pre_a(0, h); pre_b(0, h)
+        for j in range(2 if t else 0, len(SUB[0]) - 1):
             gather(t, 0, j)
         slist(t, 0)
         if t == 0:
+            slist(t, 1)
             at(2)
             late_constants()
             at(4)
         if t == 0:
             compare(t, 0, 0)
             counts(t, 0, 0)
+            gather(t, 1, 0)
+            op("V", cp(X("oS"), X("voI")), ["voI"], ["oS"])
+            send(q + 2, X("rOB"), X("oS"), "aOB", ["oS"])
         if t:
             table(("PC", "OA", "SP")[t - 1], ("rPC", "rOA", "pS")[t - 1], ("P7", "P5"))
         for j in range(1, len(SUB[0]) - 1):
             compare(t, 0, j)
             if j == len(SUB[0]) - 2:
-                pre_n(t, 1)
-                pre_u(t, 1)
+                if t:
+                    pre_n(t, 1)
+                    pre_u(t, 1)
+                    pre_z(t, 1)
             counts(t, 0, j)
-        slist(t, 1)
         if t:
+            slist(t, 1)
             scan_hi(t, 0)
-        pre_L(t, 1); pre_a(t, 1); pre_b(t, 1)
-        for j in range(len(SUB[1]) - 1):
-            gather(t, 1, j)
+            pre_L(t, 1); pre_a(t, 1); pre_b(t, 1)
+            gather(t, 1, 0)
         if t == 1:
-            shifted("PC", 1024, "L0C", 0, False, 0)
+            shifted_pe("L0C", 0, False, 0)
         if t == 2:
             resumed("L1A", "OA", "MSG0", ["lk00", "lk01"], 0)
-            shifted("OA", 1024, "L1A", 1, True, 1)
+            shifted_pe("L1A", 1, True, 1)
         if t == 3:
-            shifted("SP", 1024, "L0h", 0, False, 0)
-        if t == 0:
-            op("V", cp(X("oS"), X("voI")), ["voI"], ["oS"])
-            send(q + 2, X("rOB"), X("oS"), "aOB", ["oS"])
-            for k in range(4):
-                op("S", act(X("N%d" % k), X("it%d" % k), scale=X("m0")), ["it%d" % k, "m0"], ["N%d" % k])
+            shifted_pe("L0h", 0, False, 0)
         if t == 3:
             for h in range(2):
                 op("V", cp(X("L3h", *half(h)), X(Lk(3, h))), [Lk(3, h)], ["L3h"])
@@ -658,18 +700,33 @@ def rank_program(g, core, T, topo):
         scan_lo(t, 0)
         verdict(t, 0)
         select(t, 0)
+        for j in range(1, len(SUB[1]) - 1):
+            gather(t, 1, j)
         if t < 3:
             ulist(t)
             old(t)
-        moves_pe(t, 0)
-        compare(t, 1, 0)
-        moves_a(t, 0)
+        moves_pe(t, 0, 0, BC)
         newz_pe(t, 0)
+        moves_pe(t, 0, BC, 16)
+        compare(t, 1, 0, (0, 1))
         newz(t, 0)
+        compare(t, 1, 0, (2, 3))
+        moves_a(t, 0)
+        if t == 0:
+            number_n(0)
+        else:
+            shifted_act(("PC", "OA", "SP")[t - 1], 1024, t == 2)
         if t < 3:
             strat_pre(t, 0)
             strat_pe(t, 0)
             strat_r(t, 0)
+        if t == 0:
+            number_lo()
+            number_hi(0)
+        if t == 1:
+            for k in (1, 2, 3):
+                number_n(k)
+                number_hi(k)
         counts(t, 1, 0)
         for j in range(1, len(SUB[1]) - 1):
             compare(t, 1, j)
@@ -688,11 +745,12 @@ def rank_program(g, core, T, topo):
         if t < 3:
             number_pe(t)
             pre_n(t + 1, 0)
-        select(t, 1, True)
+        select(t, 1, t == 3)
         if t < 3:
             number(t)
             moves_pe(t, 1, 0, BC)
             pre_u(t + 1, 0)
+            pre_z(t + 1, 0)
             strat_pe(t, 1)
             newz_pe(t, 1)
             moves_pe(t, 1, BC, 16)
@@ -705,36 +763,46 @@ def rank_program(g, core, T, topo):
             moves_a(t, 1)
             compare(t + 1, 0, 0)
             counts(t + 1, 0, 0)
+            gather(t + 1, 0, 1)
+            if t == 2:
+                verdicts_home(0)
+                verdicts_home(1)
+            else:
+                list_constants(t)
             moves_b(t, 1)
             home_list(t)
             if t == 0:
                 send(q + 1, X("rOA"), X("oS"), "aOA", ["oS"])
         else:
-            moves_pe(t, 1)
+            moves_pe(t, 1, 0, 8)
+            moves_pe(t, 1, 8, 16)
             newz_pe(t, 1)
-            for k in range(3):
-                op("V", cp(X("hk", 32 * k, 32 * k + 32), X("HM%d" % k)), ["HM%d" % k], ["hk%d" % k])
-                for h in range(2):
-                    c = 32 * k + 16 * h + 8
-                    op("V", tt(X("kall", 16 * k + 8 * h, 16 * k + 8 * h + 8), X("hk", c, c + 8), X("k16"), A.subtract),
-                       ["hk%d" % k, "k16"], ["kall"])
+            moves_v(t, 1, 0, 8)
+            moves_f(t, 1, 0, 8)
+            verdicts_home(2)
+            moves_v(t, 1, 8, 16)
+            moves_f(t, 1, 8, 16)
             newz(t, 1)
-            moves_a(t, 1)
+            op("T", permuted(0, "Sh1", "L3r", 3, 3, "I1"), ["Sh1", "I1", "L3r", "Lo", "Hi3"], ["P7"])
+            op("S", act(X("yob"), X("P7", 0, 256)), ["P7"], ["yob"])
+            dma("Y", T.yo[:, :], X("yob"), ["yob"], [])
+            for k in range(2):
+                op("T", [mm(X("P%d" % k, 48 * x, 48 * x + 48), X("EX", 128 * (8 * k + x), 128 * (8 * k + x) + 128), X("kall", 0, 48))
+                         for x in range(8)],
+                   ["kall"] + ["EX%d" % x for x in range(16)], ["P%d" % k])
+                op("S", act(X("ykr", 384 * k, 384 * k + 384), X("P%d" % k, 0, 384)), ["P%d" % k], ["ykr"])
+            moves_b(t, 1)
             resumed("L2H", "SP", "HM1", ["HM1"], 1)
             shifted("SP", 1280, "L2H", 2, True, 2)
-            moves_b(t, 1)
-            list_constants()
+            op("V", cp(X("hk", 96, 112), X("HM3", 16, 32)), ["HM3o"], ["hk3"])
+            for h in range(2):
+                op("V", tt(X("kall", 48 + 8 * h, 56 + 8 * h), X("hk", 96 + 8 * h, 104 + 8 * h), X("k16"), A.subtract),
+                   ["hk3", "k16"], ["kal3"])
 
     at(50)
-    op("T", permuted(0, "Sh1", "L3r", 3, 3, "I1"), ["Sh1", "I1", "L3r", "NF3"], ["P7"])
-    op("S", act(X("yob"), X("P7", 0, 256)), ["P7"], ["yob"])
-    dma("Y", T.yo[:, :], X("yob"), ["yob"], [])
-    for k in range(2):
-        op("T", [mm(X("P%d" % k, 64 * x, 64 * x + 48), X("EX", 128 * (8 * k + x), 128 * (8 * k + x) + 128), X("kall", 0, 48))
-                 for x in range(8)],
-           ["kall"] + ["EX%d" % x for x in range(16)], ["P%d" % k])
-        op("S", act(X("ykr", 512 * k, 512 * k + 512), X("P%d" % k)), ["P%d" % k], ["ykr"])
-    op("S", act(X("ykn", 0, 768), X("ykr").indirect(X("yl", 0, 48))), ["ykr", "yl"], ["ykn"])
+    op("T", [mm(X("P2", 16 * x, 16 * x + 16), X("EX", 128 * x, 128 * x + 128), X("kall", 48, 64)) for x in range(16)],
+       ["kal3"] + ["EX%d" % x for x in range(16)], ["P2"])
+    op("S", act(X("ykn", 0, 768), X("ykr", 0, 768).indirect(X("yl", 0, 48))), ["ykr", "yl"], ["ykn"])
 
     def yp_half(h):
         a, b = half(h)
@@ -742,15 +810,9 @@ def rank_program(g, core, T, topo):
            ["SP", "HM3%d" % h, "N3"], ["ypb"])
 
     yp_half(0)
-    op("V", cp(X("hk", 96, 112), X("HM3", 16, 32)), ["HM3o"], ["hk3"])
-    for h in range(2):
-        op("V", tt(X("kall", 48 + 8 * h, 56 + 8 * h), X("hk", 96 + 8 * h, 104 + 8 * h), X("k16"), A.subtract), ["hk3", "k16"],
-           ["kal3"])
     yp_half(1)
     dma("Y", T.yz[:, :], X("zf"), ["zf0", "zf1"], [])
     dma("Y", T.yp[:, :], X("ypb"), ["ypb"], [])
-    op("T", [mm(X("P2", 16 * x, 16 * x + 16), X("EX", 128 * x, 128 * x + 128), X("kall", 48, 64)) for x in range(16)],
-       ["kal3"] + ["EX%d" % x for x in range(16)], ["P2"])
     op("S", act(X("ykr3"), X("P2", 0, 256)), ["P2"], ["ykr3"])
     op("S", act(X("ykn", 768, 1024), X("ykr3").indirect(X("yl", 48, 64))), ["ykr3", "yl"], ["ykn"])
     dma("S", T.yk[:, :], T["ykn"][0:128:16, :], ["ykn"], [])

import math
import numpy as np
from concourse.bass import DstId, RemoteDMATransfer
from concourse.mybir import dt, AluOpType, AxisListType, ActivationFunctionType

A = AluOpType
COPY = ActivationFunctionType.Copy
IDN = ActivationFunctionType.Identity
MAGIC = 12582912.0

BC = 2
SUB = {0: [0, 8, 72, 128], 1: [0, 72, 128]}


def _scratch():
    s = {}

    def sb(name, n, d):
        s[name] = ("sbuf", [128, n], d)
    f, b, i, u, h = "float32", "bfloat16", "int32", "uint16", "float16"
    sb("R", 8192, b)
    for k in range(2):
        sb("Y%d" % k, 2048, b); sb("B%d" % k, 2048, b); sb("HI%d" % k, 2048, b); sb("LO%d" % k, 2048, b)
        sb("al%d" % k, 128, u); sb("nM%d" % k, 128, f); sb("nb%d" % k, 128, b); sb("pr%d" % k, 128, f)
        sb("aI%d" % k, 128, i); sb("aJ%d" % k, 128, i); sb("rm%d" % k, 128, b); sb("st%d" % k, 128, h)
        sb("ML%d" % k, 128, h); sb("hs%d" % k, 128, b); sb("ls%d" % k, 128, b)
        sb("rn%d" % k, 128, b)
        for p in range(2):
            sb("L%d%d" % (p, k), 128, f)
    for t in range(4):
        sb("MSG%d" % t, 32, u); sb("zo%d" % t, 256, b); sb("zr%d" % t, 256, b); sb("HM%d" % t, 32, u)
        sb("it%d" % t, 256, f); sb("N%d" % t, 256, f); sb("Hi%d" % t, 256, b)
        if t:
            sb("LR%d" % t, 32, u)
        if t < 3:
            sb("rb%d" % t, 16, i)
    sb("Lo", 256, b); sb("e0", 256, b); sb("il", 256, f)
    sb("zf", 256, b); sb("rM", 128, f)
    for n in ("uI", "uJ", "uK"):
        sb(n, 16, i)
    sb("UL", 16, u); sb("old", 256, b)
    for n, w in (("OB", 1024), ("PC", 1280), ("OA", 1536), ("SP", 1792)):
        sb(n, w, f)
    for n in ("oS", "pS", "rOB", "rPC", "rOA"):
        sb(n, 1024, h)
    for n in ("vpI", "voI"):
        sb(n, 1024, i)
    sb("mvI", 16, i); sb("mvu", 16, u); sb("wI", 1, i); sb("zn", 256, b); sb("zs", 256, b)
    sb("L0n", 256, f)
    for n in ("L0h", "L0A", "L0C", "L1A", "L2H", "L3h", "L3r"):
        sb(n, 256, h)
    for n in ("ip", "p16", "pg", "i1", "i2", "i3", "i4", "i5", "i6", "i7", "cAi", "cAj"):
        sb(n, 1, i)
    for n in ("pf", "p16f", "pgf", "pg16", "p1", "p2", "k15", "k14", "m0", "m1", "wf", "ck", "cA", "cR", "f1", "f2", "f3",
              "f4", "f5", "f6", "g1", "g2", "g3", "g4", "g5", "g6", "x128"):
        sb(n, 1, f)
    sb("fr", 144, f); sb("fy", 64, f); sb("Dn", 144, b); sb("Dw", 144, b); sb("D16", 144, b)
    for n in ("I1", "I2", "I4", "I4k", "bda", "bdb", "BD", "WB", "I2e", "cr", "cu", "c32", "ones", "nones"):
        sb(n, 128, b)
    sb("ik", 128, f); sb("ck16", 128, f)
    for n in ("Sh1", "Sh2"):
        sb(n, 128, b)
    sb("EX", 2048, b); sb("ind", 16, f); sb("s0", 2048, b); sb("s1", 2048, b)
    sb("q1", 128, f); sb("Bq", 128, f); sb("Br", 128, f); sb("Bc", 128, f); sb("iy", 128, f); sb("i8", 8, f); sb("k16", 8, f)
    sb("jp", 96, f)
    sb("pl", 16, u); sb("yc", 64, i); sb("yq", 64, i); sb("ye", 64, i); sb("yb", 64, i); sb("yd", 64, i); sb("yl", 64, u)
    sb("hk", 128, f); sb("kall", 64, b)
    sb("ykr", 768, f); sb("ykr3", 256, f); sb("ykn", 1024, f); sb("ypb", 256, f); sb("yob", 256, f)
    return s


_ALL = _scratch()
_PACK = {}


def _pack():
    out, width = {}, {}
    size = {"float32": 4, "int32": 4, "bfloat16": 2, "uint16": 2, "float16": 2}
    for name, (w, sh, d) in _ALL.items():
        if sh[1] <= 256:
            al = 32 // size[d]
            o = width.get(d, 0)
            _PACK[name] = ("pk_" + d, o, sh[1])
            width[d] = o + -(-sh[1] // al) * al
        else:
            out[name] = (w, sh, d)
    for d, w in width.items():
        out["pk_" + d] = ("sbuf", [128, w], d)
    for k in range(8):
        out["P%d" % k] = ("psum", [128, 512], "float32")
    return out


SCRATCH = _pack()
_ARR = ["aL0", "az0", "aOB", "aPC", "aL0C", "aOA", "aL3"] + ["al%d%d" % (t, h) for t in (1, 2, 3) for h in (0, 1)] \
    + ["az%d%d" % (t, h) for t in (1, 2, 3, 4) for h in (0, 1)] + ["ah0", "ah1", "ah2", "ah30", "ah31", "aho"]
SEMAPHORES = ["sV", "sT", "sS", "sG", "ls"] + ["d%d" % k for k in range(20)] + _ARR


def rank_program(g, core, T, topo):
    q = T.rank_of(core)
    if q is None:
        return
    ENG = {"V": g.vector, "T": g.tensor, "S": g.scalar, "G": g, "Y": g.sync}
    QSEM = {"V": "sV", "T": "sT", "S": "sS", "G": "sG"}
    cnt = {k: 0 for k in QSEM}
    clock = {k: {} for k in ENG}
    last, readers = {}, {}
    used = {}
    dn = [0]

    def X(name, a=None, b=None, step=None, rows=None):
        buf, o, w = _PACK.get(name, (name, 0, None))
        t = T[buf]
        if w is None:
            w = t.shape[1]
        a = 0 if a is None else a
        b = w if b is None else b
        r = slice(0, 128) if rows is None else rows
        if step is None:
            return t[r, o + a:o + b]
        return t[r, o + a:o + b:step]

    def wait(qn, tok):
        sem, val, snap, _ = tok
        ck = clock[qn]
        if ck.get(sem, 0) >= val:
            return
        ENG[qn].wait_ge(T.sem[sem], val)
        ck[sem] = val
        for s, v in snap.items():
            if ck.get(s, 0) < v:
                ck[s] = v

    def before(qn, R, W):
        for k in R:
            if k in last:
                wait(qn, last[k])
            if k[0] == "P" and k[1].isdigit():
                for e, tok in readers.get(k, {}).items():
                    if e != qn:
                        wait(qn, tok)
        for k in W:
            if k in last and (last[k][3] != qn or qn == "Y"):
                wait(qn, last[k])
            for e, tok in readers.get(k, {}).items():
                if e != qn:
                    wait(qn, tok)

    def after(qn, tok, R, W):
        for k in R:
            readers.setdefault(k, {})[qn] = tok
        for k in W:
            last[k] = tok
            readers[k] = {}

    prog, cur = [], [0.0]

    def at(stage):
        cur[0] = float(stage)

    def op(*a):
        prog.append((cur[0], len(prog), op_now, a))

    def dma(*a):
        prog.append((cur[0], len(prog), dma_now, a))

    def send(*a):
        prog.append((cur[0], len(prog), send_now, a))

    def op_now(qn, calls, R, W):
        before(qn, R, W)
        calls = calls if isinstance(calls, list) else [calls]
        for c in calls:
            ins = c()
        cnt[qn] += 1
        ins.then_inc(T.sem[QSEM[qn]], 1)
        used[QSEM[qn]] = cnt[qn]
        after(qn, (QSEM[qn], cnt[qn], dict(clock[qn]), qn), R, W)

    def dma_now(qn, out, in_, R, W):
        before(qn, R, W)
        sem = "d%d" % dn[0]
        dn[0] += 1
        ENG[qn].dma_start(out, in_).then_inc(T.sem[sem], 16)
        used[sem] = 16
        after("D" + sem, (sem, 16, dict(clock[qn]), "D" + sem), R, W)

    def send_now(dst, out, in_, sem, R):
        before("G", R, [])
        c = T.cores[dst % 4]
        rid, pid = topo.addr(c)[:2]
        m = topo.mask(core, c)
        g.remote_dma(out, in_, T.sem[sem], T.sem.ls, pid, rid, m)
        used["ls"] = used.get("ls", 0) + len(topo.engines(core, c))

    def arrives(src, sem, key):
        n = len(topo.engines(T.cores[src % 4], core))
        used[sem] = n
        last[key] = (sem, n, {}, "net")
        readers[key] = {}

    V, PE, S, G = g.vector, g.tensor, g.scalar, g

    def ts(out, i, s1, s2, o0, o1=None):
        if o1 is None:
            return lambda: V.tensor_scalar(out, i, s1, None, o0)
        return lambda: V.tensor_scalar(out, i, s1, s2, o0, o1)

    def tt(out, a, b, o):
        return lambda: V.tensor_tensor(out, a, b, o)

    def cp(out, a):
        return lambda: V.tensor_copy(out, a)

    def act(out, a, f=COPY, **kw):
        return lambda: S.activation(out, a, f, **kw)

    def mm(out, l, r, st=True, sp=True):
        return lambda: PE.matmul(out, l, r, st, sp)

    def vts(o, i, s1, s2, o0, o1=None, R=()):
        rd = [i] + [s for s in (s1, s2) if isinstance(s, str)]
        f = lambda s: X(s) if isinstance(s, str) else s
        op("V", ts(X(o), X(i), f(s1), f(s2), o0, o1), rd, [o])

    at(-10)
    dma("Y", X("mvI"), T.mv[:, :], [], ["mvI"])
    dma("Y", X("vpI"), T.vp[:, :], [], ["vpI"])
    dma("S", X("zn"), T.z0[:, :], [], ["zn"])
    dma("S", X("wI"), T.wt[:, :], [], ["wI"])
    dma("Y", X("R", 0, 4096), T.strat[:, 0:4096], [], ["Ra"])
    dma("S", X("R", 4096, 8192), T.strat[:, 4096:8192], [], ["R"])
    dma("Y", X("voI"), T.vo[:, :], [], ["voI"])
    at(-9)

    def iota(name, pattern, base=0, cm=0, a=None, b=None, integer=False, key=None, early=None):
        o = X(name, a, b)
        at0 = cur[0]
        at(at0 if early is None else early)
        if integer:
            op("G", lambda: G.iota(o, pattern, base, cm), [], [key or name])
        else:
            op("G", lambda: G.iota(o, pattern, base, cm, allow_small_or_imprecise_dtypes=True), [], [key or name])
        at(at0)

    iota("ip", [[0, 1]], 0, 1, integer=True)
    iota("jp", [[128, 2], [1, 4], [64, 2]], a=0, b=16, key="jp0")
    vts("p16", "ip", 15, None, A.bitwise_and)
    vts("g1", "p16", 4.0, None, A.mult)
    op("V", cp(X("mvu"), X("mvI")), ["mvI"], ["mvu"])
    op("V", ts(X("pl"), X("jp", 0, 16), X("g1"), None, A.add), ["jp0", "g1"], ["pl"])
    op("V", cp(X("L0n"), X("vpI").indirect(X("mvu"))), ["vpI", "mvu"], ["L0n"])
    op("V", cp(X("L0h"), X("L0n").indirect(X("pl"))), ["L0n", "pl"], ["L0h"])
    op("S", act(X("zs"), X("zn").indirect(X("pl"))), ["zn", "pl"], ["zs"])
    send(q + 1, X("zr0"), X("zs"), "az0", ["zs"])
    send(q + 1, X("L0A"), X("L0h"), "aL0", ["L0h"])
    arrives(q - 1, "az0", "zr0"); arrives(q - 1, "aL0", "L0A")

    iota("fr", [[1, 144]], -16, early=-9.5)
    vts("pg", "ip", 112, None, A.bitwise_and)
    op("V", cp(X("pf"), X("ip")), ["ip"], ["pf"])
    op("V", cp(X("p16f"), X("p16")), ["p16"], ["p16f"])
    op("V", cp(X("pgf"), X("pg")), ["pg"], ["pgf"])
    op("V", cp(X("wf"), X("wI")), ["wI"], ["wf"])
    op("V", ts(X("I1"), X("fr", 16, 144), X("pf"), None, A.is_equal), ["fr", "pf"], ["I1"])
    vts("pg16", "pgf", 16.0, None, A.add)
    vts("m0", "p16f", 0.0, None, A.is_equal)
    vts("ck", "p16f", 1184.0, None, A.mult)
    fr = X("fr", 16, 144)
    op("V", ts(X("bda"), fr, X("pgf"), None, A.is_ge), ["fr", "pgf"], ["bda"])
    op("V", ts(X("bdb"), fr, X("pg16"), None, A.is_lt), ["fr", "pg16"], ["bdb"])
    op("V", tt(X("BD"), X("bda"), X("bdb"), A.mult), ["bda", "bdb"], ["BD"])
    op("S", act(X("WB"), X("BD"), scale=X("wf")), ["BD", "wf"], ["WB"])
    op("S", act(X("I4k"), X("I1"), scale=-4096.0), ["I1"], ["I4k"])
    op("V", lambda: V.memset(X("cu", rows=slice(0, 64)), -32.0), [], ["cu"])
    op("V", lambda: V.memset(X("cu", rows=slice(64, 128)), 2.0 ** -7), [], ["cu"])
    for n, v in (("ones", 1.0), ("c32", 0.25)):
        op("V", lambda n=n, v=v: V.memset(X(n), v), [], [n])
    op("V", ts(X("D16"), X("fr"), X("pgf"), None, A.is_equal), ["fr", "pgf"], ["D16"])
    op("S", act(X("Dw"), X("D16"), scale=X("wf")), ["D16", "wf"], ["Dw"])
    op("S", act(X("Dn"), X("D16"), scale=-1.0), ["D16"], ["Dn"])
    op("V", ts(X("ind"), X("fr", 16, 32), X("p16f"), None, A.is_equal), ["fr", "p16f"], ["ind"])
    for x in range(16):
        op("S", act(X("EX", 128 * x, 128 * x + 128), X("BD"), scale=X("ind", x, x + 1)), ["BD", "ind"], ["EX%d" % x])
    at(-7.5)
    op("V", cp(X("pS"), X("vpI")), ["vpI"], ["pS"])
    at(2)
    send(q + 3, X("rPC"), X("pS"), "aPC", ["pS"])
    send(q + 3, X("L0C"), X("L0h"), "aL0C", ["L0h"])
    arrives(q - 2, "aOB", "rOB"); arrives(q + 1, "aPC", "rPC"); arrives(q + 1, "aL0C", "L0C"); arrives(q - 1, "aOA", "rOA")

    at(-7)
    op("V", lambda: V.memset(X("s0"), 1.0), [], ["s0"])
    op("V", lambda: V.memset(X("s0", 0, 2048, 16), 0.0), ["s0"], ["s0"])
    at(2)
    op("S", act(X("s1"), X("s0"), IDN, bias=256.0, scale=-256.0), ["s0"], ["s1"])
    at(-7)
    op("V", lambda: V.memset(X("q1"), -10.0), [], ["q1"])
    op("V", lambda: V.memset(X("q1", 15, 128, 16), -9.0), ["q1"], ["q1"])
    iota("iy", [[16, 8], [0, 16]], early=-9.5)
    iota("i8", [[16, 8]], early=-9.5)
    vts("x128", "p16f", 128.0, None, A.mult)
    vts("Bq", "iy", "x128", 150.0, A.add, A.add)
    op("V", ts(X("Br"), X("s0", 0, 128), -30000.0, None, A.mult), ["s0"], ["Br"])
    op("V", tt(X("Bc"), X("Bq"), X("Br"), A.add), ["Bq", "Br"], ["Bc"])
    at(1)
    vts("k16", "i8", "x128", None, A.add)
    for n, v in (("cr", -3 * 2.0 ** -10), ("nones", -1.0)):
        op("V", lambda n=n, v=v: V.memset(X(n), v), [], [n])
    iota("ik", [[16, 128]], early=-9.5)
    op("S", act(X("ck16"), X("ik"), IDN, bias=X("p16f")), ["ik", "p16f"], ["ck16"])
    at(-7)
    op("S", act(X("I2"), X("I1"), scale=0.5), ["I1"], ["I2"])
    op("S", act(X("I2e"), X("I1"), scale=0.5 - 2.0 ** -9), ["I1"], ["I2e"])
    op("S", act(X("I4"), X("I1"), scale=0.25), ["I1"], ["I4"])
    pats = [[[128, 2], [1, 32], [32, 4]], [[128, 2], [1, 2], [2, 64]], [[128, 2], [1, 16], [16, 8]], [[1, 256]]]
    for t in range(4):
        at(1)
        iota("it%d" % t, pats[t], 1024 + 256 * t)

    at(1)
    vts("i1", "p16", 3, None, A.bitwise_and)
    vts("i2", "p16", 2, None, A.arith_shift_right)
    vts("i3", "p16", 7, None, A.bitwise_and)
    vts("i4", "p16", 3, None, A.arith_shift_right)
    op("V", cp(X("f2"), X("i2")), ["i2"], ["f2"])
    op("V", cp(X("f4"), X("i4")), ["i4"], ["f4"])
    vts("f1", "i1", 32.0, "f2", A.mult, A.add)
    vts("f3", "i3", 16.0, "f4", A.mult, A.add)
    vts("g2", "p16f", 2.0, None, A.mult)
    iota("jp", [[128, 2], [4, 8]], a=16, b=32, key="jp1")
    iota("jp", [[128, 2], [1, 2], [32, 4]], a=32, b=48, key="jp2")
    iota("jp", [[128, 2], [2, 8]], a=48, b=64, key="jp3")
    for t, (k, c) in enumerate(((1, "f1"), (2, "g2"), (3, "f3"))):
        op("V", ts(X("rb%d" % t), X("jp", 16 * k, 16 * k + 16), X(c), 32.0, A.add, A.mult), ["jp%d" % k, c], ["rb%d" % t])

    def late_constants():
        for n, d in (("Sh1", 1), ("Sh2", 2)):
            op("G", lambda n=n, d=d: G.affine_select(X(n), X("BD"), [[1, 128]], A.is_equal, 0.0, -d, -1), ["BD"], [n])
        iota("il", [[1, 256]])

    def number_n(k):
        op("S", act(X("N%d" % k), X("it%d" % k), scale=X("m0")), ["it%d" % k, "m0"], ["N%d" % k])

    def number_lo():
        op("S", act(X("Lo"), X("il"), scale=X("m0")), ["il", "m0"], ["Lo"])
        op("S", act(X("e0"), X("il"), IDN, scale=0.0, bias=X("m0")), ["il", "m0"], ["e0"])

    def number_hi(k):
        op("S", act(X("Hi%d" % k), X("e0"), scale=1024.0 + 256 * k), ["e0"], ["Hi%d" % k])

    for k, pat in enumerate(([[0, 2], [4, 8]], [[0, 2], [1, 4], [64, 2]], [[0, 2], [8, 8]], [[0, 2], [1, 8]])):
        iota("fy", pat, a=16 * k, b=16 * k + 16, key="fy%d" % k, early=2.5)
    iota("yb", [[16, 4], [8, 2], [0, 8]], integer=True, early=2.5)

    def verdicts_home(k):
        op("V", cp(X("hk", 32 * k, 32 * k + 32), X("HM%d" % k)), ["HM%d" % k], ["hk%d" % k])
        for h in range(2):
            c = 32 * k + 16 * h + 8
            op("V", tt(X("kall", 16 * k + 8 * h, 16 * k + 8 * h + 8), X("hk", c, c + 8), X("k16"), A.subtract),
               ["hk%d" % k, "k16"], ["kall"])

    def list_constants(part):
        if part == 0:
            vts("i5", "p16", 1, None, A.bitwise_and)
            vts("i6", "p16", 1, None, A.arith_shift_right)
            op("V", cp(X("f6"), X("i6")), ["i6"], ["f6"])
            vts("f5", "i5", 64.0, "f6", A.mult, A.add)
            vts("g3", "p16f", 8.0, None, A.mult)
            return
        for t, c in enumerate(("f1", "g1", "f5", "g3")):
            op("V", ts(X("yc", 16 * t, 16 * t + 16), X("fy", 16 * t, 16 * t + 16), X(c), None, A.add), ["fy%d" % t, c], ["yc"])
        vts("yq", "yc", 3, None, A.arith_shift_right)
        op("V", ts(X("ye", 0, 48), X("yq", 0, 48), 40.0, None, A.mult), ["yq"], ["ye"])
        op("V", ts(X("ye", 48, 64), X("yq", 48, 64), 8.0, None, A.mult), ["yq"], ["ye"])
        op("V", tt(X("yd"), X("ye"), X("yc"), A.add), ["ye", "yc"], ["yd"])
        op("V", tt(X("yq"), X("yd"), X("yb"), A.add), ["yd", "yb"], ["yq"])
        op("V", cp(X("yl", 0, 48), X("yq", 0, 48)), ["yq"], ["yl"])
        op("V", ts(X("yl", 48, 64), X("yq", 48, 64), -48.0, None, A.add), ["yq"], ["yl"])

    def half(h):
        return 128 * h, 128 * h + 128

    def zkey(t, h):
        return "zr0" if t == 0 else "zr%d%d" % (t, h)

    for t in (1, 2, 3):
        src = q - 1 if t < 3 else q + 2
        for h in range(2):
            arrives(src, "al%d%d" % (t, h), "LR%d%d" % (t, h))
            arrives(src, "az%d%d" % (t, h), "zr%d%d" % (t, h))
    for t in range(4):
        src = q + 1 + t % 3
        if t < 3:
            arrives(src, "ah%d" % t, "HM%d" % t)
        else:
            for h in range(2):
                arrives(src, "ah3%d" % h, "HM3%d" % h)
                arrives(src, "az4%d" % h, "zf%d" % h)
            arrives(src, "aL3", "L3r")
            arrives(src, "aho", "HM3o")

    def Lk(t, h):
        return "L%d%d" % (t % 2, h)

    def pre_L(t, h):
        a, b = half(h)
        k = Lk(t, h)
        if t == 0:
            op("V", cp(X(k), X("L0A", a, b)), ["L0A"], [k])
        else:
            w = ("OB", "PC", "OA")[t - 1]
            op("V", tt(X(k), X(w).indirect(X("LR%d" % t, 16 * h, 16 * h + 8)), X("N%d" % (t - 1), a, b), A.add),
               [w, "LR%d%d" % (t, h), "N%d" % (t - 1)], [k])

    def pre_n(t, h):
        a, b = half(h)
        z, zk, pu = X("zr%d" % t, a, b), zkey(t, h), "P%d" % (2 + h)
        o = X(pu, 0, 128)
        op("T", [mm(o, X("cu"), X("ones"), True, False)], ["cu", "ones"], [pu])
        op("T", [mm(o, X("WB"), z, False, True)], ["WB", zk], [pu])
        op("S", act(X("nM%d" % h), o, IDN, bias=MAGIC, scale=2.0 ** -12), [pu], ["nM%d" % h])
        op("S", act(X("nb%d" % h), X("nM%d" % h), IDN, bias=-MAGIC), ["nM%d" % h], ["nb%d" % h])

    def pre_u(t, h):
        a, b = half(h)
        z, zk, pu = X("zr%d" % t, a, b), zkey(t, h), "P%d" % (2 + h)
        o = X(pu, 128, 256)
        op("T", [mm(o, X("c32"), X("ones"), True, False), mm(o, X("WB"), z, False, False)], ["c32", "ones", "WB", zk], [pu])
        op("T", [mm(o, X("I4k"), X("nb%d" % h), False, True)], ["I4k", "nb%d" % h], [pu])

    def pre_z(t, h):
        a, b = half(h)
        op("T", [mm(X("P%d" % h, d, 512, 4), X("I1"), X("zr%d" % t, a, b)) for d in range(4)], ["I1", zkey(t, h)], ["P%d" % h])

    def slist(t, h):
        a, b = half(h)
        if t < 3:
            op("T", [mm(X("P6", 256 + 8 * h, 264 + 8 * h), X("Dw", 16 - x, 144 - x), X("zr%d" % t, a + 8 * x, a + 8 * x + 8),
                        x == 0, x == 15) for x in range(16)], ["Dw", zkey(t, h)], ["P6"])

    def pre_a(t, h):
        pu = "P%d" % (2 + h)
        op("V", tt(X("pr%d" % h), X(pu, 128, 256), X(Lk(t, h)), A.mult), [pu, Lk(t, h)], ["pr%d" % h])

    def pre_b(t, h):
        k = "cA" if t else "ck"
        op("V", ts(X("aI%d" % h), X("pr%d" % h), X(k), None, A.add), ["pr%d" % h, k], ["aI%d" % h])
        op("V", ts(X("aJ%d" % h), X("aI%d" % h), 5, 8191, A.arith_shift_right, A.bitwise_and), ["aI%d" % h], ["aJ%d" % h])
        op("V", cp(X("al%d" % h), X("aJ%d" % h)), ["aJ%d" % h], ["al%d" % h])

    def ulist(t):
        op("V", cp(X("uI"), X("P6", 256, 272)), ["P6"], ["uI"])
        vts("uJ", "uI", 31, None, A.bitwise_and)
        op("V", tt(X("uK"), X("uJ"), X("rb%d" % t), A.add), ["uJ", "rb%d" % t], ["uK"])
        op("V", cp(X("UL"), X("uK")), ["uK"], ["UL"])

    def gather(t, h, j):
        a, b = SUB[h][j], SUB[h][j + 1]
        o, i = X("Y%d" % h, 16 * a, 16 * b), X("R").indirect(X("al%d" % h, a, b))
        v = h == 0 and j == 0
        op("V" if v else "S", cp(o, i) if v else act(o, i), ["R", "Ra", "al%d" % h], ["Y%d_%d" % (h, j)])

    def compare(t, h, j, ds=(0, 1, 2, 3)):
        a, b = 16 * SUB[h][j], 16 * SUB[h][j + 1]
        for d in ds:
            op("V", tt(X("B%d" % h, a + d, b, 4), X("Y%d" % h, a + d, b, 4), X("P%d" % h, a // 4, b // 4), A.is_gt),
               ["Y%d_%d" % (h, j), "P%d" % h], ["B%d_%d" % (h, j)])

    def counts(t, h, j):
        pc = "P%d" % (4 + h)
        op("T", [mm(X(pc, 0, 128), X("Dn", 16 - x, 144 - x), X("B%d" % h, 128 * x, 128 * x + 128), x == 0, x == 15)
                 for x in range(SUB[h][j] // 8, SUB[h][j + 1] // 8)], ["Dn", "B%d_%d" % (h, j)], [pc])

    def scans(t, h):
        scan_hi(t, h)
        scan_lo(t, h)

    def scan_hi(t, h):
        yk = ["Y%d_%d" % (h, j) for j in range(len(SUB[h]) - 1)]
        op("V", lambda: V.tensor_tensor_scan(X("HI%d" % h), X("s0"), X("Y%d" % h), 0.0, A.mult, A.max), ["s0"] + yk, ["HI%d" % h])

    def scan_lo(t, h):
        yk = ["Y%d_%d" % (h, j) for j in range(len(SUB[h]) - 1)]
        op("V", lambda: V.tensor_tensor_scan(X("LO%d" % h), X("s1"), X("Y%d" % h), 0.0, A.max, A.min), ["s1"] + yk, ["LO%d" % h])

    def offs(t, h):
        c = 16 * h + 8 if t < 3 else 16 + 8 * h
        return X("MSG%d" % t, c, c + 8)

    def lmov(t, h):
        c = 16 * h if t < 3 else 8 * h
        return X("MSG%d" % t, c, c + 8)

    def verdict(t, h):
        pc = "P%d" % (4 + h)
        op("V", lambda: V.tensor_tensor_scan(X("rm%d" % h), X(pc, 0, 128), X("q1"), -9.0, A.min, A.max), [pc, "q1"], ["rm%d" % h])
        op("V", lambda: V.tensor_tensor_scan(X("st%d" % h), X("Bc"), X("rm%d" % h), 0.0, A.max, A.add), ["Bc", "rm%d" % h],
           ["st%d" % h])
        op("V", cp(offs(t, h), X("st%d" % h, 14, 128, 16)), ["st%d" % h], ["of%d%d" % (t, h)])

    def select(t, h, lo_on_v=False):
        for s, w in (("hs%d" % h, "HI%d" % h), ("ls%d" % h, "LO%d" % h)):
            i = X(w).indirect(offs(t, h))
            if lo_on_v and s[0] == "l":
                op("V", cp(X(s), i), [w, "of%d%d" % (t, h)], [s])
            else:
                op("S", act(X(s), i), [w, "of%d%d" % (t, h)], [s])

    def newz_pe(t, h):
        pu = "P%d" % (2 + h)
        o = X(pu, 256, 384)
        op("T", [mm(o, X("I2"), X("ls%d" % h), True, False)], ["I2", "ls%d" % h], [pu])
        op("T", [mm(o, X("I2e"), X("hs%d" % h), False, True)], ["I2e", "hs%d" % h], [pu])

    def rounded(h, out, in_, ki, ko):
        if ko == "rn0":
            m = "rM"
            op("S", act(X(m), in_, IDN, bias=MAGIC), [ki], [m])
            op("S", act(out, X(m), IDN, bias=-MAGIC), [m], [ko])
        else:
            op("V", ts(out, in_, MAGIC, MAGIC, A.add, A.subtract), [ki], [ko])

    def newz(t, h):
        a, b = half(h)
        pu = "P%d" % (2 + h)
        o = X(pu, 256, 384)
        rounded(h, X("zo%d" % t, a, b), o, pu, "zo%d%d" % (t, h))
        if t < 3:
            send(q + 1 if t < 2 else q + 2, X("zr%d" % (t + 1), a, b), X("zo%d" % t, a, b), "az%d%d" % (t + 1, h), ["zo%d%d" % (t, h)])
        else:
            send(q - 1, X("zf", a, b), X("zo3", a, b), "az4%d" % h, ["zo3%d" % h])

    def moves_pe(t, h, a=0, b=16):
        pc = "P%d" % (4 + h)
        op("T", [mm(X(pc, 128 + 8 * x, 136 + 8 * x), X("EX", 128 * x, 128 * x + 128), X("st%d" % h, 14, 128, 16)) for x in range(a, b)],
           ["EX%d" % x for x in range(a, b)] + ["st%d" % h], [pc])

    def moves_v(t, h, a=0, b=16):
        pc = "P%d" % (4 + h)
        a, b = 8 * a, 8 * b
        op("V", tt(X(pc, 256 + a, 256 + b), X(pc, 128 + a, 128 + b), X("ck16", a, b), A.is_equal), [pc, "ck16"], [pc])
        op("V", tt(X("ML%d" % h, a, b), X(pc, 256 + a, 256 + b), X(Lk(t, h), a, b), A.mult), [pc, Lk(t, h)], ["ML%d_%d" % (h, a)])

    def moves_f(t, h, a=0, b=16):
        pc = "P%d" % (4 + h)
        op("T", [mm(X(pc, 384, 392), X("D16", 16 - x, 144 - x), X("ML%d" % h, 8 * x, 8 * x + 8), x == 0, x == 15)
                 for x in range(a, b)], ["D16", "ML%d_%d" % (h, 8 * a)], [pc])

    def moves_a(t, h):
        moves_v(t, h)
        moves_f(t, h)

    def moves_b(t, h):
        pc = "P%d" % (4 + h)
        op("V", cp(lmov(t, h), X(pc, 384, 392)), [pc], ["lk%d%d" % (t, h)])
        m = X("MSG%d" % t, 16 * h, 16 * h + 16)
        ks = ["lk%d%d" % (t, h), "of%d%d" % (t, h)]
        if t < 3:
            send(q + 1 if t < 2 else q + 2, X("LR%d" % (t + 1), 16 * h, 16 * h + 16), m, "al%d%d" % (t + 1, h), ks)
        else:
            send(q - 1, X("HM3", 8 * h, 8 * h + 8), lmov(3, h), "ah3%d" % h, ks[:1])

    def home_list(t):
        send(q - 1 - t % 3, X("HM%d" % t), X("MSG%d" % t), "ah%d" % t, ["%s%d%d" % (k, t, h) for k in ("lk", "of") for h in (0, 1)])

    def number_pe(t):
        o = X("P5", 400, 408)
        op("T", [mm(o, X("nones"), X("rm%d" % h, 14, 128, 16), h == 0, h == 1) for h in range(2)], ["nones", "rm0", "rm1"], ["P5"])

    def number(t):
        op("V", lambda: V.tensor_reduce(X("cR"), X("P5", 400, 408), AxisListType.X, A.add), ["P5"], ["cR"])
        op("V", cp(X("cAi"), X("cR")), ["cR"], ["cAi"])
        vts("cAj", "cAi", 255, None, A.bitwise_and)
        vts("cA", "cAj", 32.0, "ck", A.mult, A.add)

    def old(t):
        op("S", act(X("old"), X("R").indirect(X("UL"))), ["R", "Ra", "UL"], ["old"])

    def strat_pe(t, h):
        a, b = half(h)
        o = X("P6", a, b)
        op("T", [mm(o, X("I4"), X("ls%d" % h), False, False), mm(o, X("I4"), X("hs%d" % h), False, True)],
           ["I4", "hs%d" % h, "ls%d" % h], ["P6"])

    def strat_pre(t, h):
        a, b = half(h)
        o = X("P6", a, b)
        op("T", [mm(o, X("cr"), X("ones"), True, False), mm(o, X("I2"), X("old", a, b), False, False)],
           ["cr", "ones", "I2", "old"], ["P6"])

    def strat_r(t, h):
        a, b = half(h)
        rounded(h, X("rn%d" % h), X("P6", a, b), "P6", "rn%d" % h)

    def strat_v(t, h):
        op("V", cp(X("R").indirect(X("UL", 8 * h, 8 * h + 8)), X("rn%d" % h)), ["rn%d" % h, "UL"], ["R"])

    def table(w, r, banks=("P0", "P7")):
        for k in range(2):
            a, p = 512 * k, banks[k]
            op("T", mm(X(p), X("Sh1"), X(r, a, a + 512)), ["Sh1", r], [p])
            op("S", act(X(w, a, a + 512), X(p)), [p], [w])

    def runs(t):
        if t == 0:
            return [((32 * b, 32 * b + 32, None), (b, 128, 4)) for b in range(4)]
        if t == 1:
            return [((b, 128, 4), (32 * b, 32 * b + 32, None)) for b in range(4)]
        if t == 2:
            return [((64 * b, 64 * b + 64, None), (b, 128, 2)) for b in range(2)]
        return [((b, 128, 8), (16 * b, 16 * b + 16, None)) for b in range(8)]

    def permuted(at, sh, Lb, t, nf, shn):
        cs = []
        for h in range(2):
            for (a, b, st), (c, d, dst) in runs(t):
                o = X("P7", at + 128 * h + c, at + 128 * h + d, dst)
                cs.append((o, X(sh), X(Lb, 128 * h + a, 128 * h + b, st)))
        if nf is None:
            return [mm(*c) for c in cs]
        o = X("P7", at, at + 256)
        return [mm(o, X(shn), X("Lo"), True, False), mm(o, X(shn), X("Hi%d" % nf), False, False)] + [
            mm(*c, False, c is cs[-1]) for c in cs]

    def shifted(w, at, Lb, t, t_before, t_mover):
        shifted_pe(Lb, t, t_before, t_mover)
        shifted_act(w, at, t_before)

    def shifted_act(w, at, t_before):
        n = 512 if t_before else 256
        op("S", act(X(w, at, at + n), X("P7", 0, n)), ["P7"], [w])

    def shifted_pe(Lb, t, t_before, t_mover):
        n = 0
        cs = []
        if t_before:
            cs += permuted(0, "Sh1", Lb, t, None, None)
            n = 256
        cs += permuted(n, "Sh2", Lb, t, t_mover, "Sh1")
        op("T", cs, ["Sh1", "Sh2", Lb, "Lo", "Hi%d" % t_mover], ["P7"])

    def resumed(Lb, w, lst, keys, t):
        for h in range(2):
            a, b = half(h)
            op("V", tt(X(Lb, a, b), X(w).indirect(X(lst, 16 * h, 16 * h + 8)), X("N%d" % t, a, b), A.add),
               [w, "N%d" % t] + keys, [Lb])

    for t in range(4):
        at(0 if t == 0 else 10 * t)
        if t == 0:
            pre_L(0, 0); pre_n(0, 0); pre_n(0, 1)
            for h in range(2):
                if h:
                    pre_L(0, 1)
                pre_u(0, h); pre_z(0, h); pre_a(0, h); pre_b(0, h)
        for j in range(2 if t else 0, len(SUB[0]) - 1):
            gather(t, 0, j)
        slist(t, 0)
        if t == 0:
            slist(t, 1)
            at(2)
            late_constants()
            at(4)
        if t == 0:
            compare(t, 0, 0)
            counts(t, 0, 0)
            gather(t, 1, 0)
            op("V", cp(X("oS"), X("voI")), ["voI"], ["oS"])
            send(q + 2, X("rOB"), X("oS"), "aOB", ["oS"])
        if t:
            table(("PC", "OA", "SP")[t - 1], ("rPC", "rOA", "pS")[t - 1], ("P7", "P5"))
        for j in range(1, len(SUB[0]) - 1):
            compare(t, 0, j)
            if j == len(SUB[0]) - 2:
                if t:
                    pre_n(t, 1)
                    pre_u(t, 1)
                    pre_z(t, 1)
            counts(t, 0, j)
        if t:
            slist(t, 1)
            scan_hi(t, 0)
            pre_L(t, 1); pre_a(t, 1); pre_b(t, 1)
            gather(t, 1, 0)
        if t == 1:
            shifted_pe("L0C", 0, False, 0)
        if t == 2:
            resumed("L1A", "OA", "MSG0", ["lk00", "lk01"], 0)
            shifted_pe("L1A", 1, True, 1)
        if t == 3:
            shifted_pe("L0h", 0, False, 0)
        if t == 3:
            for h in range(2):
                op("V", cp(X("L3h", *half(h)), X(Lk(3, h))), [Lk(3, h)], ["L3h"])
            send(q - 1, X("L3r"), X("L3h"), "aL3", ["L3h"])
        if t == 0:
            scan_hi(t, 0)
        scan_lo(t, 0)
        verdict(t, 0)
        select(t, 0)
        for j in range(1, len(SUB[1]) - 1):
            gather(t, 1, j)
        if t < 3:
            ulist(t)
            old(t)
        moves_pe(t, 0, 0, BC)
        newz_pe(t, 0)
        moves_pe(t, 0, BC, 16)
        compare(t, 1, 0, (0, 1))
        newz(t, 0)
        compare(t, 1, 0, (2, 3))
        moves_a(t, 0)
        if t == 0:
            number_n(0)
        else:
            shifted_act(("PC", "OA", "SP")[t - 1], 1024, t == 2)
        if t < 3:
            strat_pre(t, 0)
            strat_pe(t, 0)
            strat_r(t, 0)
        if t == 0:
            number_lo()
            number_hi(0)
        if t == 1:
            for k in (1, 2, 3):
                number_n(k)
                number_hi(k)
        counts(t, 1, 0)
        for j in range(1, len(SUB[1]) - 1):
            compare(t, 1, j)
            counts(t, 1, j)
        moves_b(t, 0)
        if t < 3:
            strat_pre(t, 1)
        if t == 0:
            table("OB", "rOB", ("P1", "P7"))
        scans(t, 1)
        if t < 3:
            strat_v(t, 0)
        verdict(t, 1)
        if t == 3:
            send(q - 1, X("HM3", 16, 32), X("MSG3", 16, 32), "aho", ["of30", "of31"])
        if t < 3:
            number_pe(t)
            pre_n(t + 1, 0)
        select(t, 1, t == 3)
        if t < 3:
            number(t)
            moves_pe(t, 1, 0, BC)
            pre_u(t + 1, 0)
            pre_z(t + 1, 0)
            strat_pe(t, 1)
            newz_pe(t, 1)
            moves_pe(t, 1, BC, 16)
            pre_L(t + 1, 0)
            pre_a(t + 1, 0); pre_b(t + 1, 0)
            strat_r(t, 1)
            strat_v(t, 1)
            newz(t, 1)
            gather(t + 1, 0, 0)
            moves_a(t, 1)
            compare(t + 1, 0, 0)
            counts(t + 1, 0, 0)
            gather(t + 1, 0, 1)
            if t == 2:
                verdicts_home(0)
                verdicts_home(1)
            else:
                list_constants(t)
            moves_b(t, 1)
            home_list(t)
            if t == 0:
                send(q + 1, X("rOA"), X("oS"), "aOA", ["oS"])
        else:
            moves_pe(t, 1, 0, 8)
            moves_pe(t, 1, 8, 16)
            newz_pe(t, 1)
            moves_v(t, 1, 0, 8)
            moves_f(t, 1, 0, 8)
            verdicts_home(2)
            moves_v(t, 1, 8, 16)
            moves_f(t, 1, 8, 16)
            newz(t, 1)
            op("T", permuted(0, "Sh1", "L3r", 3, 3, "I1"), ["Sh1", "I1", "L3r", "Lo", "Hi3"], ["P7"])
            op("S", act(X("yob"), X("P7", 0, 256)), ["P7"], ["yob"])
            dma("Y", T.yo[:, :], X("yob"), ["yob"], [])
            for k in range(2):
                op("T", [mm(X("P%d" % k, 48 * x, 48 * x + 48), X("EX", 128 * (8 * k + x), 128 * (8 * k + x) + 128), X("kall", 0, 48))
                         for x in range(8)],
                   ["kall"] + ["EX%d" % x for x in range(16)], ["P%d" % k])
                op("S", act(X("ykr", 384 * k, 384 * k + 384), X("P%d" % k, 0, 384)), ["P%d" % k], ["ykr"])
            moves_b(t, 1)
            resumed("L2H", "SP", "HM1", ["HM1"], 1)
            shifted("SP", 1280, "L2H", 2, True, 2)
            op("V", cp(X("hk", 96, 112), X("HM3", 16, 32)), ["HM3o"], ["hk3"])
            for h in range(2):
                op("V", tt(X("kall", 48 + 8 * h, 56 + 8 * h), X("hk", 96 + 8 * h, 104 + 8 * h), X("k16"), A.subtract),
                   ["hk3", "k16"], ["kal3"])

    at(50)
    op("T", [mm(X("P2", 16 * x, 16 * x + 16), X("EX", 128 * x, 128 * x + 128), X("kall", 48, 64)) for x in range(16)],
       ["kal3"] + ["EX%d" % x for x in range(16)], ["P2"])
    op("S", act(X("ykn", 0, 768), X("ykr", 0, 768).indirect(X("yl", 0, 48))), ["ykr", "yl"], ["ykn"])

    def yp_half(h):
        a, b = half(h)
        op("V", tt(X("ypb", a, b), X("SP").indirect(X("HM3", 8 * h, 8 * h + 8)), X("N3", a, b), A.add),
           ["SP", "HM3%d" % h, "N3"], ["ypb"])

    yp_half(0)
    yp_half(1)
    dma("Y", T.yz[:, :], X("zf"), ["zf0", "zf1"], [])
    dma("Y", T.yp[:, :], X("ypb"), ["ypb"], [])
    op("S", act(X("ykr3"), X("P2", 0, 256)), ["P2"], ["ykr3"])
    op("S", act(X("ykn", 768, 1024), X("ykr3").indirect(X("yl", 48, 64))), ["ykr3", "yl"], ["ykn"])
    dma("S", T.yk[:, :], T["ykn"][0:128:16, :], ["ykn"], [])
    prog.sort(key=lambda e: e[:2])
    for _, _, f, a in prog:
        f(*a)
    for sem, v in used.items():
        if clock["G"].get(sem, 0) < v:
            g.wait_ge(T.sem[sem], v)
